import numpy as np
import ml_dtypes


def mxq(x, axis, fmt="e4m3"):
    dtype, down = {"e4m3": (ml_dtypes.float8_e4m3fn, 7), "e5m2": (ml_dtypes.float8_e5m2, 14)}[fmt]
    v = np.moveaxis(np.asarray(x, np.float32).astype(ml_dtypes.bfloat16).astype(np.float64), axis, -1)
    blocks = v.reshape(v.shape[:-1] + (-1, 32))
    amax = np.abs(blocks).max(-1, keepdims=True)
    byte = np.maximum(np.where(amax > 0, np.frexp(amax)[1] - 1 + 127, 0) - down, 1)
    scale = np.exp2(byte - 127.0)
    codes = (blocks / scale).astype(np.float32).astype(dtype).astype(np.float64)
    return np.moveaxis((codes * scale).reshape(v.shape), -1, axis)


WIDE = False


def mx_kscale(k):
    if not WIDE:
        return np.ones(k)
    levels = np.array([10, -10, 5, -5, 0])
    if k % 512:
        return np.exp2(np.random.permutation(np.resize(levels, k // 32))).repeat(32)
    a = np.empty((k // 512, 16))
    for p in range(k // 512):
        a[p, :8] = np.random.permutation(np.resize(levels, 8))
        for g in range(8):
            far = levels[np.abs(levels - a[p, g]) >= 10]
            a[p, g + 8] = far[np.random.randint(len(far))]
    return np.exp2(a.ravel()).repeat(32)


BF16 = ml_dtypes.bfloat16


def bf(x):
    return np.asarray(x, np.float32).astype(BF16)


def f64(x):
    return np.asarray(x).astype(np.float64)


E2M1 = np.array([0.0, 0.5, 1.0, 1.5, 2.0, 3.0, 4.0, 6.0, -0.0, -0.5, -1.0, -1.5, -2.0, -3.0, -4.0, -6.0])


def pack_weight(w, fmt):
    k, n = w.shape
    w = f64(bf(w)).reshape(k // 32, 32, n)
    amax = np.abs(w).max(1)
    if fmt == "e4m3":
        byte = np.frexp(amax)[1] - 1 + 127 - 7
    else:
        mant, ex = np.frexp(amax / 6.0)
        byte = np.where(mant > 0.5, ex, ex - 1) + 127
    byte = np.clip(np.where(amax > 0, byte, 1), 1, 254)
    scaled = (w * np.exp2(127.0 - byte)[:, None, :]).reshape(k, n).astype(np.float32)
    by_word = np.ascontiguousarray(scaled.reshape(k // 512, 128, 4, n).transpose(0, 1, 3, 2))
    if fmt == "e4m3":
        words = by_word.astype(ml_dtypes.float8_e4m3fn).view(np.uint8)
    else:
        c = by_word.astype(ml_dtypes.float4_e2m1fn).view(np.uint8) & 0xF
        words = c[..., 0::2] | (c[..., 1::2] << 4)
    return np.ascontiguousarray(words), np.ascontiguousarray(byte.astype(np.uint8).reshape(k // 512, 16, n))


def unpack_weight(words, scales, fmt):
    g, p, n, _ = words.shape
    if fmt == "e4m3":
        vals = np.ascontiguousarray(words).view(ml_dtypes.float8_e4m3fn).astype(np.float64)
    else:
        nib = np.empty((g, p, n, 4), np.uint8)
        nib[..., 0::2] = words & 0xF
        nib[..., 1::2] = words >> 4
        vals = E2M1[nib]
    vals = vals * np.repeat(np.exp2(scales.astype(np.float64) - 127.0), 8, axis=1)[..., None]
    return vals.transpose(0, 1, 3, 2).reshape(g * 512, n)
def pack4(w):
    words, scales = pack_weight(w, "e2m1")
    return words.reshape(words.shape[0], 128, -1), scales


def unpack4(words, scales):
    return unpack_weight(words.reshape(words.shape[0], 128, -1, 2), scales, "e2m1")


def planes(Y):
    n, m = Y.shape
    b = f64(bf(Y)).reshape(n // 32, 32, m)
    amax = np.abs(b).max(1)
    byte = np.clip(np.where(amax > 0, np.frexp(amax)[1] - 1 + 127 - 7, 1), 1, 254)
    codes = (b * np.exp2(127.0 - byte)[:, None, :]).reshape(n, m).astype(np.float32).astype(ml_dtypes.float8_e4m3fn).view(np.uint8)
    words = codes.reshape(n // 512, 128, 4, m).transpose(0, 1, 3, 2)
    return np.ascontiguousarray(words), np.ascontiguousarray(byte.astype(np.uint8).reshape(n // 512, 16, m))


B, F, KC, KT, D = 128, 8, 512, 1024, 2048

def setup_inputs():
    sc = mx_kscale(KC)
    st = mx_kscale(KT)
    cls = np.random.randn(B, KC)
    tim = np.random.randn(B, F, KT)
    wc = np.random.randn(KC, D) / np.sqrt(KC)
    wt = np.random.randn(KT, D) / np.sqrt(KT)
    class_w_words, class_w_scales = pack4(wc / sc[:, None])
    time_w_words, time_w_scales = pack4(wt / st[:, None])
    return {
        "class_features": bf(cls * sc),
        "time_features": bf(tim * st),
        "class_w_words": class_w_words,
        "class_w_scales": class_w_scales,
        "time_w_words": time_w_words,
        "time_w_scales": time_w_scales,
        "bias": bf(0.3 * np.random.randn(D)),
        "gain": bf(np.exp(0.8 * np.random.randn(D))),
    }

def reference(class_features, time_features, class_w_words, class_w_scales, time_w_words, time_w_scales, bias, gain):
    wc = unpack4(class_w_words, class_w_scales)
    pc = mxq(f64(class_features), 1, "e4m3") @ wc
    wt = unpack4(time_w_words, time_w_scales)
    pt = mxq(f64(time_features).reshape(B * F, KT), 1, "e4m3") @ wt
    z = pt.reshape(B, F, D) + pc.reshape(B, 1, D) + f64(bias)
    y = z / (1.0 + np.exp(-z)) * f64(gain)
    words, scales = planes(y.reshape(B * F, D).T)
    return y, words, scales

@@ -1,0 +1,553 @@
+from contextlib import ExitStack
+
+import concourse.mybir as mybir
+from concourse.masks import make_identity
+
+B, F, KC, KT, D = 128, 8, 512, 1024, 2048
+FLOPS = 2 * B * KC * D + 2 * B * F * KT * D
+
+F32 = mybir.dt.float32
+BF16 = mybir.dt.bfloat16
+U32 = mybir.dt.uint32
+I32 = mybir.dt.int32
+U8 = mybir.dt.uint8
+FP8X4 = mybir.dt.float8_e4m3fn_x4
+FP4X4 = mybir.dt.float4_e2m1fn_x4
+ALU = mybir.AluOpType
+ACT = mybir.ActivationFunctionType
+
+P = 128
+GW = 512
+G = D // GW
+PAIRS = G * F // 2
+TURNED = {}
+ORDER = [(0, 0), (1, 0), (0, 1), (1, 1), (0, 2), (1, 2), (0, 3), (1, 3)] + [(g, k) for g in (2, 3) for k in range(4)]
+CAST = "sssssssvsssssvsv"
+
+
+def tile_clip_class_timestep_condition_g4_kernel(
+    tc, class_features, time_features, class_w_words, class_w_scales, time_w_words, time_w_scales, bias, gain, out_0, out_1, out_2
+):
+    nc = tc.nc
+    with ExitStack() as ctx:
+        keep = ctx.enter_context(tc.tile_pool(name="keep", bufs=1))
+        ring = ctx.enter_context(tc.tile_pool(name="ring", bufs=3))
+        psum = ctx.enter_context(tc.psum_pool(name="psum", bufs=8))
+        ctx.enter_context(tc.manual_schedule())
+
+        def bank():
+            return psum.tile([P, GW], F32, name="bank", tag="bank")
+
+        ident = keep.tile([P, P], F32, name="ident")
+        cls_sb = keep.tile([P, KC], BF16, name="cls_sb")
+        tim_sb = keep.tile([P, F, KT], BF16, name="tim_sb")
+        wc_words = keep.tile([P, 2 * D], U8, name="wc_words", align_bytes=64)
+        wt_words = keep.tile([P, 2, 2 * D], U8, name="wt_words", align_bytes=64)
+        wc_plane = keep.tile([P, D], U8, name="wc_plane", align_bytes=64)
+        wt_plane = keep.tile([P, 2, D], U8, name="wt_plane", align_bytes=64)
+        vec_rows = keep.tile([16, P], BF16, name="vec_rows")
+        vec_square = keep.tile([P, P], F32, name="vec_square")
+        vec_cols = keep.tile([P, 16], F32, name="vec_cols")
+        warm = keep.tile([P, 8], F32, name="warm")
+        gain_rows = keep.tile([P, D], BF16, name="gain_rows")
+        bias_rows = keep.tile([P, D], BF16, name="bias_rows")
+        pcb = keep.tile([P, D], F32, name="pcb")
+        cls_grouped = keep.tile([P, B, 2], F32, name="cls_grouped", align_bytes=64)
+        reps = 4 if TURNED else 1
+        cls_codes = keep.tile([P, reps * B], U32, name="cls_codes", align_bytes=64)
+        cls_plane = keep.tile([P, reps * B], U8, name="cls_plane", align_bytes=64)
+        tim_codes = keep.tile([P, 2, F * B], U32, name="tim_codes", align_bytes=64)
+        tim_plane = keep.tile([P, 2, F * B], U8, name="tim_plane", align_bytes=64)
+        out_plane = keep.tile([P, B * F], U8, name="out_plane", align_bytes=64)
+
+        wc_hbm = class_w_words[0].bitcast(I32)
+        wt_hbm = time_w_words.rearrange("s p n -> p s n").bitcast(I32)
+        cs_hbm = class_w_scales[0].bitcast(I32)
+        ts_hbm = time_w_scales.rearrange("s q n -> q s n").bitcast(I32)
+        words_hbm = out_1.rearrange("g p m t -> g p (m t)").bitcast(I32)
+        scales_hbm = out_2.bitcast(I32)
+
+        banks = {}
+        tiles = {}
+
+        def turn_class():
+            bk = bank()
+            words = cls_sb[:].bitcast(F32)
+            for u in range(2):
+                nc.tensor.transpose(bk[:, u * B : (u + 1) * B], words[:, u : KC // 2 : 2], ident[:])
+            banks["cls"] = bk
+
+        def copy_class():
+            nc.vector.tensor_copy(out=cls_grouped[:], in_=banks["cls"][:, 0 : 2 * B].rearrange("p (u b) -> p b u", u=2))
+
+        def quant_class(r):
+            cols = slice(r * B, (r + 1) * B)
+            nc.vector.quantize_mx(
+                out=cls_codes[:, cols].bitcast(FP8X4),
+                scales=cls_plane[:, cols],
+                in_=cls_grouped[:].rearrange("p b u -> p (b u)").bitcast(BF16),
+            )
+
+        def turn_frame(f):
+            bk = bank()
+            words = tim_sb[:, f, :].bitcast(F32)
+            for s in range(2):
+                for u in range(2):
+                    k = 2 * s + u
+                    nc.tensor.transpose(bk[:, k * B : (k + 1) * B], words[:, 256 * s + u : 256 * (s + 1) : 2], ident[:])
+            banks["frame", f] = bk
+
+        def copy_frame(f, eng):
+            grouped = ring.tile([P, 2, B, 2], F32, name="frame_grouped", tag="frame_grouped", bufs=8, align_bytes=64)
+            src = banks["frame", f][:].rearrange("p (s u b) -> p s b u", s=2, u=2)
+            if eng == "s":
+                nc.scalar.copy(out=grouped[:], in_=src)
+            else:
+                nc.vector.tensor_copy(out=grouped[:], in_=src)
+            tiles["frame", f] = grouped
+
+        def quant_frame(f):
+            cols = slice(f * B, (f + 1) * B)
+            for s in range(2):
+                nc.vector.quantize_mx(
+                    out=tim_codes[:, s, cols].bitcast(FP8X4),
+                    scales=tim_plane[:, s, cols],
+                    in_=tiles["frame", f][:, s, :, :].rearrange("p b u -> p (b u)").bitcast(BF16),
+                )
+
+        def class_product(g):
+            bk = bank()
+            nc.tensor.matmul_mx(
+                out=bk[:],
+                lhsT=cls_codes[:, 0:B].bitcast(FP8X4),
+                lhsT_scale=cls_plane[:, 0:B],
+                rhs=wc_words[:, 2 * GW * g : 2 * GW * (g + 1)].bitcast(FP4X4),
+                rhs_scale=wc_plane[:, GW * g : GW * (g + 1)],
+                start=True,
+                stop=True,
+            )
+            banks["pc", g] = bk
+
+        def add_bias(g):
+            nc.vector.tensor_tensor(out=pcb[:, g * GW : (g + 1) * GW], in0=banks["pc", g][:], in1=bias_rows[:, g * GW : (g + 1) * GW], op=ALU.add)
+
+        def is_turned(j):
+            return (ORDER[j][0], ORDER[j][1] // 2) in TURNED
+
+        def time_product(j, i):
+            g = ORDER[j][0]
+            f = 2 * ORDER[j][1] + i
+            bk = bank()
+            for s in range(2):
+                nc.tensor.matmul_mx(
+                    out=bk[:],
+                    lhsT=tim_codes[:, s, f * B : (f + 1) * B].bitcast(FP8X4),
+                    lhsT_scale=tim_plane[:, s, f * B : (f + 1) * B],
+                    rhs=wt_words[:, s, 2 * GW * g : 2 * GW * (g + 1)].bitcast(FP4X4),
+                    rhs_scale=wt_plane[:, s, GW * g : GW * (g + 1)],
+                    start=(s == 0),
+                    stop=(s == 1),
+                )
+            banks["unit", j, i] = bk
+
+        def chunk_product(g, h, c):
+            bk = bank()
+            d0 = GW * g + P * c
+            toks = slice(4 * B * h, 4 * B * (h + 1))
+            nc.tensor.matmul_mx(
+                out=bk[:],
+                lhsT=wc_words[:, 2 * d0 : 2 * (d0 + P)].bitcast(FP4X4),
+                lhsT_scale=wc_plane[:, d0 : d0 + P],
+                rhs=cls_codes[:].bitcast(FP8X4),
+                rhs_scale=cls_plane[:],
+                start=True,
+                stop=False,
+            )
+            for s in range(2):
+                nc.tensor.matmul_mx(
+                    out=bk[:],
+                    lhsT=wt_words[:, s, 2 * d0 : 2 * (d0 + P)].bitcast(FP4X4),
+                    lhsT_scale=wt_plane[:, s, d0 : d0 + P],
+                    rhs=tim_codes[:, s, toks].bitcast(FP8X4),
+                    rhs_scale=tim_plane[:, s, toks],
+                    start=False,
+                    stop=(s == 1),
+                )
+            banks["chunk", g, h, c] = bk
+
+        def chunk_silu(g, h, c):
+            if c == 0:
+                tiles["turned", g, h] = ring.tile([P, 4, GW], F32, name="turned", tag="turned", bufs=2)
+            k = 4 * g + c
+            nc.scalar.activation(
+                out=tiles["turned", g, h][:, c, :], in_=banks["chunk", g, h, c][:], func=ACT.Silu, bias=vec_cols[:, k : k + 1]
+            )
+
+        def turn_back(j, i):
+            g, h = ORDER[j][0], ORDER[j][1] // 2
+            fl = 2 * (ORDER[j][1] % 2) + i
+            bk = bank()
+            for c in range(4):
+                nc.tensor.transpose(bk[:, c * P : (c + 1) * P], tiles["turned", g, h][:, c, fl * B : (fl + 1) * B], ident[:])
+            banks["unit", j, i] = bk
+
+        def pair_tile(kind, j, depth):
+            if (kind, j) not in tiles:
+                tiles[kind, j] = ring.tile([P, 2, GW], F32, name=kind, tag=kind, bufs=depth)
+            return tiles[kind, j]
+
+        def empty_unit(j, i):
+            cols = slice(ORDER[j][0] * GW, (ORDER[j][0] + 1) * GW)
+            if is_turned(j):
+                nc.vector.tensor_tensor(out=pair_tile("y", j, 10)[:, i, :], in0=banks["unit", j, i][:], in1=gain_rows[:, cols], op=ALU.mult)
+            else:
+                nc.vector.tensor_tensor(out=pair_tile("z", j, 5)[:, i, :], in0=banks["unit", j, i][:], in1=pcb[:, cols], op=ALU.add)
+
+        def silu(j, i0, i1):
+            z = tiles["z", j][:, i0:i1, :].rearrange("p i d -> p (i d)")
+            nc.scalar.activation(out=z, in_=z, func=ACT.Silu)
+
+        def apply_gain(j, i0, i1):
+            cols = slice(ORDER[j][0] * GW, (ORDER[j][0] + 1) * GW)
+            nc.vector.tensor_tensor(
+                out=pair_tile("y", j, 10)[:, i0:i1, :],
+                in0=tiles["z", j][:, i0:i1, :],
+                in1=gain_rows[:, cols].unsqueeze(1).to_broadcast([P, i1 - i0, GW]),
+                op=ALU.mult,
+            )
+
+        def store_y(j, i0, i1):
+            g, f0 = ORDER[j][0], 2 * ORDER[j][1]
+            nc.sync.dma_start(out=out_0[:, f0 + i0 : f0 + i1, g * GW : (g + 1) * GW], in_=tiles["y", j][:, i0:i1, :])
+
+        def cast(j, i0, i1, eng):
+            if ("yb", j) not in tiles:
+                tiles["yb", j] = ring.tile([P, 2, 2 * P, 2], BF16, name="yb", tag="yb", bufs=8)
+            dst = tiles["yb", j][:, :, i0 * P : i1 * P, :]
+            src = tiles["y", j][:, i0:i1, :].rearrange("b i (p u e) -> b u (i p) e", u=2, e=2)
+            if eng == "g":
+                nc.gpsimd.tensor_scalar(out=dst, in0=src, scalar1=1.0, scalar2=1.0, op0=ALU.mult, op1=ALU.mult)
+            elif eng == "s":
+                nc.scalar.copy(out=dst, in_=src)
+            else:
+                nc.vector.tensor_copy(out=dst, in_=src)
+
+        def turn_y(j, i0, i1):
+            if ("yt", j) not in banks:
+                banks["yt", j] = bank()
+            words = tiles["yb", j][:].rearrange("b u c e -> b (u c e)").bitcast(F32)
+            for i in range(i0, i1):
+                for u in range(2):
+                    k = 2 * u + i
+                    nc.tensor.transpose(banks["yt", j][:, k * P : (k + 1) * P], words[:, k * P : (k + 1) * P], ident[:])
+
+        def copy_y(j, b0, b1, eng):
+            g, f0 = ORDER[j][0], 2 * ORDER[j][1]
+            if ("grouped", g) not in tiles:
+                tiles["grouped", g] = ring.tile([P, B, F, 2], F32, name="grouped", tag="grouped", bufs=4, align_bytes=64)
+            dst = tiles["grouped", g][:, b0:b1, f0 : f0 + 2, :]
+            src = banks["yt", j][:].rearrange("p (u i b) -> p b i u", u=2, i=2)[:, b0:b1, :, :]
+            if eng == "s":
+                nc.scalar.copy(out=dst, in_=src)
+            else:
+                nc.vector.tensor_copy(out=dst, in_=src)
+
+        def quant_y(g, m0, m1):
+            if ("codes", g) not in tiles:
+                tiles["codes", g] = ring.tile([P, B * F], U32, name="codes", tag="codes", bufs=4, align_bytes=64)
+            src = tiles["grouped", g][:].rearrange("p b f u -> p (b f u)").bitcast(BF16)
+            nc.vector.quantize_mx(
+                out=tiles["codes", g][:, m0:m1].bitcast(FP8X4), scales=out_plane[4 * g : P, m0:m1], in_=src[:, 4 * m0 : 4 * m1]
+            )
+
+        def store_codes(g, m0, m1):
+            nc.sync.dma_start(out=words_hbm[g, :, m0:m1], in_=tiles["codes", g][:, m0:m1].bitcast(I32))
+
+        def store_scales(q):
+            nc.sync.dma_start(out=scales_hbm[:, 4 * q : 4 * q + 4, :], in_=out_plane[:].bitcast(I32)[32 * q : 32 * q + 16, :])
+
+        def load_frames(f0, f1):
+            nc.sync.dma_start(out=tim_sb[:, f0:f1, :], in_=time_features[:, f0:f1, :])
+
+        def load_wc(g0, g1):
+            cols = slice(256 * g0, 256 * g1)
+            nc.sync.dma_start(out=wc_words[:].bitcast(I32)[:, cols], in_=wc_hbm[:, cols])
+
+        def load_wt(g0, g1):
+            cols = slice(256 * g0, 256 * g1)
+            nc.sync.dma_start(out=wt_words[:].bitcast(I32)[:, :, cols], in_=wt_hbm[:, :, cols])
+
+        def load_cs(g0, g1):
+            cols = slice(128 * g0, 128 * g1)
+            for q in range(4):
+                nc.sync.dma_start(out=wc_plane[:].bitcast(I32)[32 * q : 32 * q + 4, cols], in_=cs_hbm[4 * q : 4 * q + 4, cols])
+
+        def load_ts(g0, g1):
+            cols = slice(128 * g0, 128 * g1)
+            for q in range(4):
+                nc.sync.dma_start(out=wt_plane[:].bitcast(I32)[32 * q : 32 * q + 4, :, cols], in_=ts_hbm[4 * q : 4 * q + 4, :, cols])
+
+        def load_rows(queue, rows, vec, g0, g1):
+            cols = slice(GW * g0, GW * g1)
+            queue.dma_start(out=rows[:, cols], in_=vec[cols].partition_broadcast(P))
+
+        def turn_bias():
+            bk = bank()
+            nc.tensor.transpose(bk[:, 0:P], vec_square[:], ident[:])
+            banks["vec"] = bk
+
+        def widen_bias():
+            nc.vector.tensor_copy(out=vec_square[0:16, :], in_=vec_rows[:])
+
+        def copy_bias_cols():
+            nc.scalar.copy(out=vec_cols[:], in_=banks["vec"][:, 0:16])
+
+        nc.vector.memset(warm[:], 0.0)
+        nc.vector.memset(wc_plane[:].bitcast(I32), 0)
+        nc.vector.memset(ident[:], 0.0)
+        nc.vector.memset(wt_plane[:].rearrange("p s n -> p (s n)").bitcast(I32), 0)
+        make_identity(nc, ident[:], True)
+        nc.scalar.activation(out=warm[:], in_=warm[:], func=ACT.Silu)
+        load_rows(nc.gpsimd, bias_rows, bias, 0, 2)
+        load_rows(nc.gpsimd, gain_rows, gain, 0, 2)
+        load_frames(0, 1)
+        nc.sync.dma_start(out=cls_sb[:], in_=class_features)
+        load_wc(0, 2)
+        load_frames(1, 2)
+        load_cs(0, 2)
+        load_ts(0, 2)
+        load_wt(0, 1)
+        load_wt(1, 2)
+        load_frames(2, 4)
+        load_frames(4, 6)
+        load_frames(6, 8)
+        load_cs(2, G)
+        load_ts(2, G)
+        load_wc(2, G)
+        load_rows(nc.sync, bias_rows, bias, 2, G)
+        load_wt(2, G)
+        load_rows(nc.sync, gain_rows, gain, 2, G)
+
+        turn_frame(0)
+        turn_class()
+        copy_frame(0, 's')
+        turn_frame(1)
+        copy_class()
+        quant_frame(0)
+        quant_class(0)
+        copy_frame(1, 's')
+        class_product(0)
+        class_product(1)
+        quant_frame(1)
+        add_bias(0)
+        time_product(0, 0)
+        add_bias(1)
+        time_product(0, 1)
+        empty_unit(0, 0)
+        turn_frame(2)
+        empty_unit(0, 1)
+        time_product(1, 0)
+        copy_frame(2, 's')
+        time_product(1, 1)
+        silu(0, 0, 2)
+        empty_unit(1, 0)
+        turn_frame(3)
+        quant_frame(2)
+        turn_frame(4)
+        empty_unit(1, 1)
+        copy_frame(3, 's')
+        apply_gain(0, 0, 2)
+        time_product(2, 0)
+        silu(1, 0, 2)
+        time_product(3, 0)
+        quant_frame(3)
+        turn_frame(5)
+        store_y(0, 0, 2)
+        empty_unit(2, 0)
+        copy_frame(4, 's')
+        time_product(2, 1)
+        apply_gain(1, 0, 2)
+        cast(0, 0, 2, 's')
+        time_product(3, 1)
+        empty_unit(2, 1)
+        copy_frame(5, 's')
+        store_y(1, 0, 2)
+        turn_y(0, 0, 2)
+        quant_frame(4)
+        cast(1, 0, 2, 's')
+        turn_frame(6)
+        quant_frame(5)
+        empty_unit(3, 0)
+        time_product(4, 0)
+        silu(2, 0, 2)
+        empty_unit(3, 1)
+        time_product(4, 1)
+        empty_unit(4, 0)
+        time_product(5, 0)
+        copy_y(0, 0, 128, 's')
+        empty_unit(4, 1)
+        time_product(5, 1)
+        silu(3, 0, 2)
+        apply_gain(2, 0, 2)
+        turn_frame(7)
+        turn_y(1, 0, 2)
+        copy_frame(6, 's')
+        empty_unit(5, 0)
+        store_y(2, 0, 2)
+        cast(2, 0, 2, 's')
+        apply_gain(3, 0, 2)
+        copy_frame(7, 's')
+        quant_frame(6)
+        turn_y(2, 0, 2)
+        store_y(3, 0, 2)
+        empty_unit(5, 1)
+        copy_y(1, 0, 128, 's')
+        quant_frame(7)
+        time_product(6, 0)
+        silu(4, 0, 2)
+        cast(3, 0, 2, 's')
+        time_product(6, 1)
+        apply_gain(4, 0, 2)
+        time_product(7, 0)
+        time_product(7, 1)
+        copy_y(2, 0, 128, 's')
+        empty_unit(6, 0)
+        class_product(2)
+        store_y(4, 0, 2)
+        silu(5, 0, 2)
+        empty_unit(6, 1)
+        turn_y(3, 0, 2)
+        add_bias(2)
+        time_product(8, 0)
+        cast(4, 0, 2, 's')
+        time_product(8, 1)
+        apply_gain(5, 0, 2)
+        time_product(9, 0)
+        copy_y(3, 0, 128, 's')
+        empty_unit(7, 0)
+        turn_y(4, 0, 2)
+        store_y(5, 0, 2)
+        silu(6, 0, 2)
+        empty_unit(7, 1)
+        time_product(10, 0)
+        empty_unit(8, 0)
+        time_product(9, 1)
+        cast(5, 0, 2, 's')
+        apply_gain(6, 0, 2)
+        time_product(10, 1)
+        copy_y(4, 0, 128, 's')
+        empty_unit(8, 1)
+        turn_y(5, 0, 2)
+        store_y(6, 0, 2)
+        silu(7, 0, 2)
+        empty_unit(9, 0)
+        time_product(11, 1)
+        empty_unit(9, 1)
+        time_product(11, 0)
+        cast(6, 0, 2, 's')
+        apply_gain(7, 0, 2)
+        class_product(3)
+        copy_y(5, 0, 128, 's')
+        empty_unit(10, 0)
+        turn_y(6, 0, 2)
+        store_y(7, 0, 2)
+        silu(8, 0, 2)
+        cast(7, 0, 2, 'v')
+        time_product(12, 0)
+        empty_unit(10, 1)
+        time_product(12, 1)
+        copy_y(6, 0, 128, 's')
+        apply_gain(8, 0, 2)
+        silu(9, 0, 2)
+        turn_y(7, 0, 2)
+        time_product(13, 0)
+        quant_y(0, 0, 512)
+        store_y(8, 0, 2)
+        cast(8, 0, 2, 's')
+        add_bias(3)
+        store_codes(0, 0, 512)
+        apply_gain(9, 0, 2)
+        time_product(14, 0)
+        copy_y(7, 0, 128, 's')
+        silu(10, 0, 2)
+        turn_y(8, 0, 2)
+        empty_unit(11, 0)
+        store_y(9, 0, 2)
+        time_product(14, 1)
+        empty_unit(11, 1)
+        cast(9, 0, 2, 's')
+        time_product(13, 1)
+        quant_y(0, 512, 1024)
+        quant_y(1, 0, 512)
+        store_codes(0, 512, 1024)
+        copy_y(8, 0, 128, 's')
+        apply_gain(10, 0, 2)
+        turn_y(9, 0, 2)
+        store_codes(1, 0, 512)
+        silu(11, 0, 2)
+        time_product(15, 1)
+        empty_unit(12, 0)
+        store_y(10, 0, 2)
+        cast(10, 0, 2, 's')
+        empty_unit(12, 1)
+        quant_y(1, 512, 1024)
+        time_product(15, 0)
+        copy_y(9, 0, 128, 's')
+        apply_gain(11, 0, 2)
+        store_codes(1, 512, 1024)
+        silu(12, 0, 2)
+        turn_y(10, 0, 2)
+        empty_unit(13, 0)
+        store_y(11, 0, 2)
+        cast(11, 0, 2, 's')
+        empty_unit(13, 1)
+        apply_gain(12, 0, 2)
+        copy_y(10, 0, 128, 's')
+        turn_y(11, 0, 2)
+        silu(13, 0, 2)
+        empty_unit(14, 0)
+        store_y(12, 0, 2)
+        empty_unit(14, 1)
+        cast(12, 0, 2, 's')
+        empty_unit(15, 0)
+        apply_gain(13, 0, 2)
+        copy_y(11, 0, 128, 's')
+        turn_y(12, 0, 2)
+        silu(14, 0, 2)
+        empty_unit(15, 1)
+        store_y(13, 0, 2)
+        cast(13, 0, 2, 'v')
+        copy_y(12, 0, 128, 's')
+        quant_y(2, 0, 512)
+        turn_y(13, 0, 2)
+        silu(15, 0, 2)
+        apply_gain(14, 0, 2)
+        store_codes(2, 0, 512)
+        copy_y(13, 0, 128, 's')
+        quant_y(2, 512, 1024)
+        store_y(14, 0, 2)
+        cast(14, 0, 2, 's')
+        apply_gain(15, 0, 2)
+        store_codes(2, 512, 1024)
+        turn_y(14, 0, 2)
+        cast(15, 0, 1, 'v')
+        store_y(15, 0, 1)
+        store_y(15, 1, 2)
+        cast(15, 1, 2, 'v')
+        turn_y(15, 0, 1)
+        copy_y(14, 0, 128, 's')
+        turn_y(15, 1, 2)
+        copy_y(15, 0, 64, 's')
+        copy_y(15, 64, 128, 's')
+        quant_y(3, 0, 256)
+        quant_y(3, 256, 512)
+        quant_y(3, 512, 768)
+        store_codes(3, 0, 256)
+        quant_y(3, 768, 1024)
+        store_codes(3, 256, 512)
+        store_codes(3, 512, 768)
+        store_codes(3, 768, 1024)
+        store_scales(0)
+        store_scales(1)
+        store_scales(2)
+        store_scales(3)

@@ -20,9 +20,9 @@ P = 128
 GW = 512
 G = D // GW
 PAIRS = G * F // 2
-TURNED = {}
+TURNED = {(2, 1): [5, 6, 7, 8], (3, 1): [9, 10, 11, 12]}
 ORDER = [(0, 0), (1, 0), (0, 1), (1, 1), (0, 2), (1, 2), (0, 3), (1, 3)] + [(g, k) for g in (2, 3) for k in range(4)]
-CAST = "sssssssvsssssvsv"
+CAST = "x"
 
 
 def tile_clip_class_timestep_condition_g4_kernel(
@@ -38,6 +38,9 @@ def tile_clip_class_timestep_condition_g4_kernel(
         def bank():
             return psum.tile([P, GW], F32, name="bank", tag="bank")
 
+        def bank_bf():
+            return psum.tile([P, 2 * GW], BF16, name="bank_bf", tag="bank")
+
         ident = keep.tile([P, P], F32, name="ident")
         cls_sb = keep.tile([P, KC], BF16, name="cls_sb")
         tim_sb = keep.tile([P, F, KT], BF16, name="tim_sb")
@@ -45,12 +48,14 @@ def tile_clip_class_timestep_condition_g4_kernel(
         wt_words = keep.tile([P, 2, 2 * D], U8, name="wt_words", align_bytes=64)
         wc_plane = keep.tile([P, D], U8, name="wc_plane", align_bytes=64)
         wt_plane = keep.tile([P, 2, D], U8, name="wt_plane", align_bytes=64)
-        vec_rows = keep.tile([16, P], BF16, name="vec_rows")
-        vec_square = keep.tile([P, P], F32, name="vec_square")
-        vec_cols = keep.tile([P, 16], F32, name="vec_cols")
+        ident_bf = keep.tile([P, P], BF16, name="ident_bf")
+        vec_squares = [keep.tile([P, P], BF16, name="bias_square"), keep.tile([P, P], BF16, name="gain_square")]
+        vec_cols = keep.tile([P, 2, 16], BF16, name="vec_cols")
+        tim_grouped = keep.tile([P, F // 2, 2, 2, B, 2], F32, name="tim_grouped", align_bytes=64)
         warm = keep.tile([P, 8], F32, name="warm")
-        gain_rows = keep.tile([P, D], BF16, name="gain_rows")
         bias_rows = keep.tile([P, D], BF16, name="bias_rows")
+        gain_rows = keep.tile([P, D], BF16, name="gain_rows")
+        vec_rows = [bias_rows, gain_rows]
         pcb = keep.tile([P, D], F32, name="pcb")
         cls_grouped = keep.tile([P, B, 2], F32, name="cls_grouped", align_bytes=64)
         reps = 4 if TURNED else 1
@@ -77,8 +82,14 @@ def tile_clip_class_timestep_condition_g4_kernel(
                 nc.tensor.transpose(bk[:, u * B : (u + 1) * B], words[:, u : KC // 2 : 2], ident[:])
             banks["cls"] = bk
 
-        def copy_class():
-            nc.vector.tensor_copy(out=cls_grouped[:], in_=banks["cls"][:, 0 : 2 * B].rearrange("p (u b) -> p b u", u=2))
+        def move(eng, dst, src):
+            if eng == "s":
+                nc.scalar.copy(out=dst, in_=src)
+            else:
+                nc.vector.tensor_copy(out=dst, in_=src)
+
+        def copy_class(eng):
+            move(eng, cls_grouped[:], banks["cls"][:, 0 : 2 * B].rearrange("p (u b) -> p b u", u=2))
 
         def quant_class(r):
             cols = slice(r * B, (r + 1) * B)
@@ -98,22 +109,40 @@ def tile_clip_class_timestep_condition_g4_kernel(
             banks["frame", f] = bk
 
         def copy_frame(f, eng):
-            grouped = ring.tile([P, 2, B, 2], F32, name="frame_grouped", tag="frame_grouped", bufs=8, align_bytes=64)
+            dst = tim_grouped[:, f // 2, :, f % 2, :, :]
             src = banks["frame", f][:].rearrange("p (s u b) -> p s b u", s=2, u=2)
             if eng == "s":
-                nc.scalar.copy(out=grouped[:], in_=src)
+                nc.scalar.copy(out=dst, in_=src)
             else:
-                nc.vector.tensor_copy(out=grouped[:], in_=src)
-            tiles["frame", f] = grouped
+                nc.vector.tensor_copy(out=dst, in_=src)
 
-        def quant_frame(f):
-            cols = slice(f * B, (f + 1) * B)
+        def quant_frames(f0, f1):
+            cols = slice(f0 * B, f1 * B)
             for s in range(2):
+                src = tim_grouped[:, f0 // 2, s, f0 % 2 : f0 % 2 + f1 - f0, :, :]
                 nc.vector.quantize_mx(
                     out=tim_codes[:, s, cols].bitcast(FP8X4),
                     scales=tim_plane[:, s, cols],
-                    in_=tiles["frame", f][:, s, :, :].rearrange("p b u -> p (b u)").bitcast(BF16),
+                    in_=src.rearrange("p i b u -> p (i b u)").bitcast(BF16),
                 )
+
+        def turn_vec(which):
+            bk = bank_bf()
+            nc.tensor.transpose(bk[:, 0:P], vec_squares[which][:], ident_bf[:])
+            banks["vec", which] = bk
+
+        def copy_vec(which, eng):
+            move(eng, vec_cols[:, which, :], banks["vec", which][:, 0:16])
+
+        def spread(which, g0, g1):
+            bk = bank_bf()
+            for c in range(4 * (g1 - g0)):
+                k = 4 * g0 + c
+                nc.tensor.transpose(bk[:, c * P : (c + 1) * P], vec_cols[:, which, k : k + 1].to_broadcast([P, P]), ident_bf[:])
+            banks["spread", which, g0] = bk
+
+        def copy_rows(which, g0, g1, eng):
+            move(eng, vec_rows[which][:, g0 * GW : g1 * GW], banks["spread", which, g0][:, 0 : (g1 - g0) * GW])
 
         def class_product(g):
             bk = bank()
@@ -176,11 +205,11 @@ def tile_clip_class_timestep_condition_g4_kernel(
             banks["chunk", g, h, c] = bk
 
         def chunk_silu(g, h, c):
-            if c == 0:
-                tiles["turned", g, h] = ring.tile([P, 4, GW], F32, name="turned", tag="turned", bufs=2)
+            if ("turned", g, h) not in tiles:
+                tiles["turned", g, h] = ring.tile([P, 4, GW], F32, name="turned", tag="turned", bufs=3)
             k = 4 * g + c
             nc.scalar.activation(
-                out=tiles["turned", g, h][:, c, :], in_=banks["chunk", g, h, c][:], func=ACT.Silu, bias=vec_cols[:, k : k + 1]
+                out=tiles["turned", g, h][:, c, :], in_=banks["chunk", g, h, c][:], func=ACT.Silu, bias=vec_cols[:, 0, k : k + 1]
             )
 
         def turn_back(j, i):
@@ -199,7 +228,7 @@ def tile_clip_class_timestep_condition_g4_kernel(
         def empty_unit(j, i):
             cols = slice(ORDER[j][0] * GW, (ORDER[j][0] + 1) * GW)
             if is_turned(j):
-                nc.vector.tensor_tensor(out=pair_tile("y", j, 10)[:, i, :], in0=banks["unit", j, i][:], in1=gain_rows[:, cols], op=ALU.mult)
+                nc.vector.tensor_tensor(out=pair_tile("y", j, 9)[:, i, :], in0=banks["unit", j, i][:], in1=gain_rows[:, cols], op=ALU.mult)
             else:
                 nc.vector.tensor_tensor(out=pair_tile("z", j, 5)[:, i, :], in0=banks["unit", j, i][:], in1=pcb[:, cols], op=ALU.add)
 
@@ -210,7 +239,7 @@ def tile_clip_class_timestep_condition_g4_kernel(
         def apply_gain(j, i0, i1):
             cols = slice(ORDER[j][0] * GW, (ORDER[j][0] + 1) * GW)
             nc.vector.tensor_tensor(
-                out=pair_tile("y", j, 10)[:, i0:i1, :],
+                out=pair_tile("y", j, 9)[:, i0:i1, :],
                 in0=tiles["z", j][:, i0:i1, :],
                 in1=gain_rows[:, cols].unsqueeze(1).to_broadcast([P, i1 - i0, GW]),
                 op=ALU.mult,
@@ -254,7 +283,7 @@ def tile_clip_class_timestep_condition_g4_kernel(
 
         def quant_y(g, m0, m1):
             if ("codes", g) not in tiles:
-                tiles["codes", g] = ring.tile([P, B * F], U32, name="codes", tag="codes", bufs=4, align_bytes=64)
+                tiles["codes", g] = ring.tile([P, B * F], U32, name="codes", tag="codes", bufs=3, align_bytes=64)
             src = tiles["grouped", g][:].rearrange("p b f u -> p (b f u)").bitcast(BF16)
             nc.vector.quantize_mx(
                 out=tiles["codes", g][:, m0:m1].bitcast(FP8X4), scales=out_plane[4 * g : P, m0:m1], in_=src[:, 4 * m0 : 4 * m1]
@@ -287,267 +316,300 @@ def tile_clip_class_timestep_condition_g4_kernel(
             for q in range(4):
                 nc.sync.dma_start(out=wt_plane[:].bitcast(I32)[32 * q : 32 * q + 4, :, cols], in_=ts_hbm[4 * q : 4 * q + 4, :, cols])
 
-        def load_rows(queue, rows, vec, g0, g1):
-            cols = slice(GW * g0, GW * g1)
-            queue.dma_start(out=rows[:, cols], in_=vec[cols].partition_broadcast(P))
+        def load_vec(which):
+            nc.sync.dma_start(out=vec_squares[which][0:16, :], in_=[bias, gain][which].rearrange("(c p) -> c p", p=P))
 
-        def turn_bias():
-            bk = bank()
-            nc.tensor.transpose(bk[:, 0:P], vec_square[:], ident[:])
-            banks["vec"] = bk
+        def fill(k):
+            nc.vector.memset([warm[:], vec_squares[0][:], vec_squares[1][:], ident[:]][k], 0.0)
 
-        def widen_bias():
-            nc.vector.tensor_copy(out=vec_square[0:16, :], in_=vec_rows[:])
+        def fill_plane(k):
+            nc.vector.memset([wc_plane[:], wt_plane[:].rearrange("p s n -> p (s n)")][k].bitcast(I32), 0)
 
-        def copy_bias_cols():
-            nc.scalar.copy(out=vec_cols[:], in_=banks["vec"][:, 0:16])
+        def build_ident():
+            make_identity(nc, ident[:], True)
 
-        nc.vector.memset(warm[:], 0.0)
-        nc.vector.memset(wc_plane[:].bitcast(I32), 0)
-        nc.vector.memset(ident[:], 0.0)
-        nc.vector.memset(wt_plane[:].rearrange("p s n -> p (s n)").bitcast(I32), 0)
-        make_identity(nc, ident[:], True)
-        nc.scalar.activation(out=warm[:], in_=warm[:], func=ACT.Silu)
-        load_rows(nc.gpsimd, bias_rows, bias, 0, 2)
-        load_rows(nc.gpsimd, gain_rows, gain, 0, 2)
-        load_frames(0, 1)
-        nc.sync.dma_start(out=cls_sb[:], in_=class_features)
-        load_wc(0, 2)
+        def narrow_ident():
+            nc.vector.tensor_copy(out=ident_bf[:], in_=ident[:])
+
+        def warm_up():
+            nc.scalar.activation(out=warm[:], in_=warm[:], func=ACT.Silu)
+
+        def load_class():
+            nc.sync.dma_start(out=cls_sb[:], in_=class_features)
+
+        fill(1)
+        load_class()
         load_frames(1, 2)
+        fill(3)
+        load_frames(0, 1)
+        fill_plane(0)
+        fill(2)
+        fill_plane(1)
         load_cs(0, 2)
-        load_ts(0, 2)
+        load_vec(0)
+        build_ident()
+        load_wc(0, 2)
+        narrow_ident()
+        turn_class()
         load_wt(0, 1)
+        turn_frame(1)
+        copy_class('s')
+        load_ts(0, 2)
+        quant_class(2)
+        load_vec(1)
+        turn_vec(0)
+        load_wc(2, 4)
+        turn_frame(0)
+        fill(0)
+        quant_class(0)
+        copy_frame(1, 'v')
+        copy_vec(0, 's')
+        load_ts(2, 4)
+        warm_up()
+        spread(0, 0, 1)
+        quant_frames(1, 2)
+        copy_frame(0, 'v')
+        class_product(0)
         load_wt(1, 2)
         load_frames(2, 4)
-        load_frames(4, 6)
-        load_frames(6, 8)
-        load_cs(2, G)
-        load_ts(2, G)
-        load_wc(2, G)
-        load_rows(nc.sync, bias_rows, bias, 2, G)
-        load_wt(2, G)
-        load_rows(nc.sync, gain_rows, gain, 2, G)
-
-        turn_frame(0)
-        turn_class()
-        copy_frame(0, 's')
-        turn_frame(1)
-        copy_class()
-        quant_frame(0)
-        quant_class(0)
-        copy_frame(1, 's')
-        class_product(0)
-        class_product(1)
-        quant_frame(1)
-        add_bias(0)
-        time_product(0, 0)
-        add_bias(1)
+        load_cs(2, 4)
+        copy_rows(0, 0, 1, 's')
         time_product(0, 1)
-        empty_unit(0, 0)
-        turn_frame(2)
+        quant_frames(0, 1)
+        add_bias(0)
+        load_frames(4, 6)
+        class_product(1)
+        load_frames(6, 8)
         empty_unit(0, 1)
-        time_product(1, 0)
-        copy_frame(2, 's')
+        time_product(0, 0)
+        load_wt(2, 4)
+        turn_vec(1)
+        spread(0, 1, 2)
+        empty_unit(0, 0)
         time_product(1, 1)
+        copy_vec(1, 's')
+        copy_rows(0, 1, 2, 's')
+        quant_class(3)
+        time_product(1, 0)
         silu(0, 0, 2)
-        empty_unit(1, 0)
-        turn_frame(3)
-        quant_frame(2)
-        turn_frame(4)
+        add_bias(1)
+        spread(1, 0, 2)
         empty_unit(1, 1)
-        copy_frame(3, 's')
+        turn_frame(2)
+        copy_rows(1, 0, 2, 's')
+        turn_frame(3)
+        empty_unit(1, 0)
+        copy_frame(2, 's')
+        turn_frame(4)
         apply_gain(0, 0, 2)
-        time_product(2, 0)
-        silu(1, 0, 2)
-        time_product(3, 0)
-        quant_frame(3)
+        copy_frame(3, 's')
         turn_frame(5)
+        silu(1, 0, 2)
+        quant_frames(2, 4)
         store_y(0, 0, 2)
-        empty_unit(2, 0)
+        time_product(3, 1)
+        copy_frame(5, 'v')
         copy_frame(4, 's')
-        time_product(2, 1)
         apply_gain(1, 0, 2)
         cast(0, 0, 2, 's')
-        time_product(3, 1)
-        empty_unit(2, 1)
-        copy_frame(5, 's')
-        store_y(1, 0, 2)
-        turn_y(0, 0, 2)
-        quant_frame(4)
-        cast(1, 0, 2, 's')
-        turn_frame(6)
-        quant_frame(5)
-        empty_unit(3, 0)
-        time_product(4, 0)
-        silu(2, 0, 2)
+        time_product(3, 0)
         empty_unit(3, 1)
-        time_product(4, 1)
-        empty_unit(4, 0)
-        time_product(5, 0)
-        copy_y(0, 0, 128, 's')
-        empty_unit(4, 1)
-        time_product(5, 1)
+        cast(1, 0, 2, 's')
+        store_y(1, 0, 2)
+        turn_frame(6)
+        empty_unit(3, 0)
+        time_product(2, 0)
+        quant_frames(4, 6)
         silu(3, 0, 2)
-        apply_gain(2, 0, 2)
-        turn_frame(7)
-        turn_y(1, 0, 2)
+        time_product(2, 1)
+        empty_unit(2, 0)
+        time_product(5, 1)
+        empty_unit(2, 1)
         copy_frame(6, 's')
-        empty_unit(5, 0)
-        store_y(2, 0, 2)
-        cast(2, 0, 2, 's')
+        time_product(5, 0)
         apply_gain(3, 0, 2)
-        copy_frame(7, 's')
-        quant_frame(6)
-        turn_y(2, 0, 2)
-        store_y(3, 0, 2)
-        empty_unit(5, 1)
-        copy_y(1, 0, 128, 's')
-        quant_frame(7)
-        time_product(6, 0)
-        silu(4, 0, 2)
+        time_product(4, 1)
+        silu(2, 0, 2)
+        turn_y(0, 0, 2)
+        time_product(4, 0)
+        empty_unit(5, 0)
         cast(3, 0, 2, 's')
-        time_product(6, 1)
-        apply_gain(4, 0, 2)
-        time_product(7, 0)
-        time_product(7, 1)
-        copy_y(2, 0, 128, 's')
-        empty_unit(6, 0)
+        store_y(3, 0, 2)
+        empty_unit(4, 1)
+        turn_frame(7)
+        empty_unit(5, 1)
+        spread(1, 2, 4)
+        copy_y(0, 0, 128, 's')
+        empty_unit(4, 0)
+        spread(0, 2, 4)
+        copy_frame(7, 's')
         class_product(2)
-        store_y(4, 0, 2)
+        apply_gain(2, 0, 2)
+        silu(4, 0, 2)
+        time_product(8, 0)
+        quant_frames(6, 8)
+        copy_rows(0, 2, 4, 's')
+        store_y(2, 0, 2)
+        time_product(6, 0)
+        quant_class(1)
+        apply_gain(4, 0, 2)
+        copy_rows(1, 2, 4, 's')
+        time_product(7, 1)
         silu(5, 0, 2)
+        add_bias(2)
+        time_product(6, 1)
+        store_y(4, 0, 2)
+        turn_y(1, 0, 2)
+        empty_unit(6, 0)
+        cast(2, 0, 2, 's')
+        time_product(7, 0)
         empty_unit(6, 1)
         turn_y(3, 0, 2)
-        add_bias(2)
-        time_product(8, 0)
-        cast(4, 0, 2, 's')
-        time_product(8, 1)
-        apply_gain(5, 0, 2)
-        time_product(9, 0)
-        copy_y(3, 0, 128, 's')
-        empty_unit(7, 0)
-        turn_y(4, 0, 2)
-        store_y(5, 0, 2)
-        silu(6, 0, 2)
-        empty_unit(7, 1)
-        time_product(10, 0)
         empty_unit(8, 0)
-        time_product(9, 1)
-        cast(5, 0, 2, 's')
+        cast(4, 0, 2, 's')
+        chunk_product(2, 1, 1)
+        empty_unit(7, 1)
+        empty_unit(7, 0)
+        silu(6, 0, 2)
+        chunk_product(2, 1, 2)
+        apply_gain(5, 0, 2)
+        chunk_product(2, 1, 3)
+        chunk_silu(2, 1, 2)
+        copy_y(3, 0, 128, 'v')
+        chunk_product(2, 1, 0)
+        copy_y(1, 0, 128, 's')
+        store_y(5, 0, 2)
         apply_gain(6, 0, 2)
-        time_product(10, 1)
-        copy_y(4, 0, 128, 's')
-        empty_unit(8, 1)
-        turn_y(5, 0, 2)
-        store_y(6, 0, 2)
         silu(7, 0, 2)
-        empty_unit(9, 0)
-        time_product(11, 1)
-        empty_unit(9, 1)
-        time_product(11, 0)
-        cast(6, 0, 2, 's')
-        apply_gain(7, 0, 2)
         class_product(3)
-        copy_y(5, 0, 128, 's')
-        empty_unit(10, 0)
-        turn_y(6, 0, 2)
-        store_y(7, 0, 2)
-        silu(8, 0, 2)
-        cast(7, 0, 2, 'v')
-        time_product(12, 0)
-        empty_unit(10, 1)
-        time_product(12, 1)
-        copy_y(6, 0, 128, 's')
-        apply_gain(8, 0, 2)
-        silu(9, 0, 2)
-        turn_y(7, 0, 2)
-        time_product(13, 0)
-        quant_y(0, 0, 512)
-        store_y(8, 0, 2)
-        cast(8, 0, 2, 's')
+        time_product(8, 1)
+        time_product(9, 1)
         add_bias(3)
-        store_codes(0, 0, 512)
-        apply_gain(9, 0, 2)
-        time_product(14, 0)
-        copy_y(7, 0, 128, 's')
-        silu(10, 0, 2)
-        turn_y(8, 0, 2)
+        chunk_silu(2, 1, 1)
+        store_y(6, 0, 2)
+        turn_y(2, 0, 2)
+        empty_unit(8, 1)
+        chunk_silu(2, 1, 0)
+        time_product(9, 0)
+        apply_gain(7, 0, 2)
+        silu(8, 0, 2)
+        chunk_product(3, 1, 0)
+        empty_unit(9, 0)
+        chunk_silu(2, 1, 3)
+        store_y(7, 0, 2)
+        cast(5, 0, 1, 'v')
+        copy_y(2, 0, 128, 's')
+        cast(6, 0, 2, 'v')
+        turn_back(11, 0)
+        chunk_silu(3, 1, 0)
+        empty_unit(9, 1)
+        turn_y(4, 0, 2)
+        time_product(12, 1)
+        cast(7, 0, 1, 's')
+        apply_gain(8, 0, 2)
+        time_product(12, 0)
+        silu(9, 0, 2)
+        chunk_product(3, 1, 1)
         empty_unit(11, 0)
-        store_y(9, 0, 2)
-        time_product(14, 1)
-        empty_unit(11, 1)
-        cast(9, 0, 2, 's')
-        time_product(13, 1)
-        quant_y(0, 512, 1024)
-        quant_y(1, 0, 512)
-        store_codes(0, 512, 1024)
-        copy_y(8, 0, 128, 's')
-        apply_gain(10, 0, 2)
-        turn_y(9, 0, 2)
-        store_codes(1, 0, 512)
-        silu(11, 0, 2)
-        time_product(15, 1)
+        store_y(8, 0, 2)
+        copy_y(4, 0, 128, 's')
+        cast(5, 1, 2, 'v')
+        turn_y(6, 0, 2)
+        cast(7, 1, 2, 'v')
+        cast(8, 0, 2, 's')
+        turn_back(10, 1)
         empty_unit(12, 0)
+        turn_back(10, 0)
+        chunk_product(3, 1, 2)
+        empty_unit(12, 1)
+        copy_y(6, 0, 128, 's')
+        apply_gain(9, 0, 2)
+        turn_y(7, 0, 2)
+        silu(12, 0, 2)
+        turn_back(11, 1)
+        turn_y(5, 0, 2)
+        empty_unit(10, 0)
+        chunk_silu(3, 1, 1)
+        quant_y(0, 0, 512)
+        copy_y(7, 0, 128, 's')
+        empty_unit(10, 1)
+        time_product(13, 0)
+        store_codes(0, 0, 512)
+        copy_y(5, 0, 128, 's')
+        quant_y(0, 512, 1024)
+        time_product(13, 1)
         store_y(10, 0, 2)
         cast(10, 0, 2, 's')
-        empty_unit(12, 1)
-        quant_y(1, 512, 1024)
-        time_product(15, 0)
-        copy_y(9, 0, 128, 's')
-        apply_gain(11, 0, 2)
-        store_codes(1, 512, 1024)
-        silu(12, 0, 2)
-        turn_y(10, 0, 2)
+        store_y(9, 0, 2)
+        apply_gain(12, 0, 2)
+        chunk_product(3, 1, 3)
+        chunk_silu(3, 1, 2)
+        empty_unit(11, 1)
+        store_y(12, 0, 2)
+        chunk_silu(3, 1, 3)
+        turn_back(14, 0)
         empty_unit(13, 0)
         store_y(11, 0, 2)
-        cast(11, 0, 2, 's')
+        store_codes(0, 512, 1024)
+        cast(11, 0, 1, 's')
         empty_unit(13, 1)
-        apply_gain(12, 0, 2)
-        copy_y(10, 0, 128, 's')
-        turn_y(11, 0, 2)
-        silu(13, 0, 2)
+        turn_y(8, 0, 2)
+        cast(9, 1, 2, 's')
+        cast(9, 0, 1, 'v')
+        turn_back(15, 0)
         empty_unit(14, 0)
-        store_y(12, 0, 2)
-        empty_unit(14, 1)
+        turn_back(14, 1)
         cast(12, 0, 2, 's')
+        turn_y(10, 0, 2)
         empty_unit(15, 0)
+        empty_unit(14, 1)
+        silu(13, 0, 2)
+        cast(11, 1, 2, 'v')
+        turn_y(11, 0, 2)
+        store_y(14, 0, 2)
+        cast(14, 0, 2, 'v')
+        store_y(15, 0, 1)
+        cast(15, 0, 1, 's')
+        turn_y(9, 0, 2)
+        quant_y(1, 512, 1024)
+        copy_y(8, 0, 128, 's')
+        turn_back(15, 1)
         apply_gain(13, 0, 2)
+        store_codes(1, 512, 1024)
         copy_y(11, 0, 128, 's')
         turn_y(12, 0, 2)
-        silu(14, 0, 2)
-        empty_unit(15, 1)
-        store_y(13, 0, 2)
-        cast(13, 0, 2, 'v')
-        copy_y(12, 0, 128, 's')
-        quant_y(2, 0, 512)
-        turn_y(13, 0, 2)
-        silu(15, 0, 2)
-        apply_gain(14, 0, 2)
-        store_codes(2, 0, 512)
-        copy_y(13, 0, 128, 's')
-        quant_y(2, 512, 1024)
-        store_y(14, 0, 2)
-        cast(14, 0, 2, 's')
-        apply_gain(15, 0, 2)
-        store_codes(2, 512, 1024)
+        copy_y(10, 0, 128, 's')
+        quant_y(1, 0, 512)
         turn_y(14, 0, 2)
-        cast(15, 0, 1, 'v')
-        store_y(15, 0, 1)
-        store_y(15, 1, 2)
-        cast(15, 1, 2, 'v')
+        store_y(13, 0, 2)
+        cast(13, 0, 1, 's')
+        empty_unit(15, 1)
         turn_y(15, 0, 1)
+        store_codes(1, 0, 512)
+        copy_y(9, 0, 128, 's')
+        cast(13, 1, 2, 'v')
+        turn_y(13, 0, 2)
+        store_y(15, 1, 2)
+        copy_y(12, 0, 128, 'v')
+        cast(15, 1, 2, 's')
+        quant_y(2, 0, 512)
         copy_y(14, 0, 128, 's')
         turn_y(15, 1, 2)
-        copy_y(15, 0, 64, 's')
-        copy_y(15, 64, 128, 's')
+        quant_y(2, 512, 1024)
+        copy_y(13, 0, 128, 's')
+        store_codes(2, 0, 512)
+        copy_y(15, 0, 64, 'v')
+        store_codes(2, 512, 1024)
         quant_y(3, 0, 256)
+        copy_y(15, 64, 128, 's')
         quant_y(3, 256, 512)
-        quant_y(3, 512, 768)
         store_codes(3, 0, 256)
         quant_y(3, 768, 1024)
         store_codes(3, 256, 512)
-        store_codes(3, 512, 768)
+        quant_y(3, 512, 768)
         store_codes(3, 768, 1024)
-        store_scales(0)
+        store_codes(3, 512, 768)
         store_scales(1)
-        store_scales(2)
         store_scales(3)
+        store_scales(0)
+        store_scales(2)

@@ -20,9 +20,10 @@ P = 128
 GW = 512
 G = D // GW
 PAIRS = G * F // 2
-TURNED = {(2, 1): [5, 6, 7, 8], (3, 1): [9, 10, 11, 12]}
-ORDER = [(0, 0), (1, 0), (0, 1), (1, 1), (0, 2), (1, 2), (0, 3), (1, 3)] + [(g, k) for g in (2, 3) for k in range(4)]
-CAST = "x"
+TURNED = {(3, 0): [2, 3, 4, 4], (3, 1): [6.5, 7, 8, 8.2], (2, 1): [10, 11, 12, 12]}
+ORDER = [(0, 0), (1, 0), (0, 1), (1, 1), (0, 2), (1, 2), (3, 0), (0, 3), (3, 1), (1, 3), (3, 2), (2, 0), (3, 3), (2, 1), (2, 2), (2, 3)]
+SORTED = []
+CAST = "hhhhhhhhhhhhhhhv"
 
 
 def tile_clip_class_timestep_condition_g4_kernel(
@@ -50,6 +51,7 @@ def tile_clip_class_timestep_condition_g4_kernel(
         wt_plane = keep.tile([P, 2, D], U8, name="wt_plane", align_bytes=64)
         ident_bf = keep.tile([P, P], BF16, name="ident_bf")
         vec_squares = [keep.tile([P, P], BF16, name="bias_square"), keep.tile([P, P], BF16, name="gain_square")]
+        tim_sorted = keep.tile([P, max(len(SORTED), 1), KT // 2], F32, name="tim_sorted")
         vec_cols = keep.tile([P, 2, 16], BF16, name="vec_cols")
         tim_grouped = keep.tile([P, F // 2, 2, 2, B, 2], F32, name="tim_grouped", align_bytes=64)
         warm = keep.tile([P, 8], F32, name="warm")
@@ -105,7 +107,11 @@ def tile_clip_class_timestep_condition_g4_kernel(
             for s in range(2):
                 for u in range(2):
                     k = 2 * s + u
-                    nc.tensor.transpose(bk[:, k * B : (k + 1) * B], words[:, 256 * s + u : 256 * (s + 1) : 2], ident[:])
+                    if f in SORTED:
+                        src = tim_sorted[:, SORTED.index(f), k * P : (k + 1) * P]
+                    else:
+                        src = words[:, 256 * s + u : 256 * (s + 1) : 2]
+                    nc.tensor.transpose(bk[:, k * B : (k + 1) * B], src, ident[:])
             banks["frame", f] = bk
 
         def copy_frame(f, eng):
@@ -220,27 +226,32 @@ def tile_clip_class_timestep_condition_g4_kernel(
                 nc.tensor.transpose(bk[:, c * P : (c + 1) * P], tiles["turned", g, h][:, c, fl * B : (fl + 1) * B], ident[:])
             banks["unit", j, i] = bk
 
-        def pair_tile(kind, j, depth):
-            if (kind, j) not in tiles:
-                tiles[kind, j] = ring.tile([P, 2, GW], F32, name=kind, tag=kind, bufs=depth)
-            return tiles[kind, j]
+        def y_tile(j):
+            if ("y", j) not in tiles:
+                tiles["y", j] = keep.tile([P, 2, GW], F32, name="y%d" % j)
+            return tiles["y", j]
+
+        def yb_tile(j):
+            if ("yb", j) not in tiles:
+                tiles["yb", j] = keep.tile([P, 2, 2 * P, 2], BF16, name="yb", tag="yb%d" % (j % 8))
+            return tiles["yb", j]
 
         def empty_unit(j, i):
             cols = slice(ORDER[j][0] * GW, (ORDER[j][0] + 1) * GW)
             if is_turned(j):
-                nc.vector.tensor_tensor(out=pair_tile("y", j, 9)[:, i, :], in0=banks["unit", j, i][:], in1=gain_rows[:, cols], op=ALU.mult)
+                nc.vector.tensor_tensor(out=y_tile(j)[:, i, :], in0=banks["unit", j, i][:], in1=gain_rows[:, cols], op=ALU.mult)
             else:
-                nc.vector.tensor_tensor(out=pair_tile("z", j, 5)[:, i, :], in0=banks["unit", j, i][:], in1=pcb[:, cols], op=ALU.add)
+                nc.vector.tensor_tensor(out=y_tile(j)[:, i, :], in0=banks["unit", j, i][:], in1=pcb[:, cols], op=ALU.add)
 
         def silu(j, i0, i1):
-            z = tiles["z", j][:, i0:i1, :].rearrange("p i d -> p (i d)")
+            z = tiles["y", j][:, i0:i1, :].rearrange("p i d -> p (i d)")
             nc.scalar.activation(out=z, in_=z, func=ACT.Silu)
 
         def apply_gain(j, i0, i1):
             cols = slice(ORDER[j][0] * GW, (ORDER[j][0] + 1) * GW)
             nc.vector.tensor_tensor(
-                out=pair_tile("y", j, 9)[:, i0:i1, :],
-                in0=tiles["z", j][:, i0:i1, :],
+                out=y_tile(j)[:, i0:i1, :],
+                in0=tiles["y", j][:, i0:i1, :],
                 in1=gain_rows[:, cols].unsqueeze(1).to_broadcast([P, i1 - i0, GW]),
                 op=ALU.mult,
             )
@@ -250,9 +261,7 @@ def tile_clip_class_timestep_condition_g4_kernel(
             nc.sync.dma_start(out=out_0[:, f0 + i0 : f0 + i1, g * GW : (g + 1) * GW], in_=tiles["y", j][:, i0:i1, :])
 
         def cast(j, i0, i1, eng):
-            if ("yb", j) not in tiles:
-                tiles["yb", j] = ring.tile([P, 2, 2 * P, 2], BF16, name="yb", tag="yb", bufs=8)
-            dst = tiles["yb", j][:, :, i0 * P : i1 * P, :]
+            dst = yb_tile(j)[:, :, i0 * P : i1 * P, :]
             src = tiles["y", j][:, i0:i1, :].rearrange("b i (p u e) -> b u (i p) e", u=2, e=2)
             if eng == "g":
                 nc.gpsimd.tensor_scalar(out=dst, in0=src, scalar1=1.0, scalar2=1.0, op0=ALU.mult, op1=ALU.mult)
@@ -283,7 +292,7 @@ def tile_clip_class_timestep_condition_g4_kernel(
 
         def quant_y(g, m0, m1):
             if ("codes", g) not in tiles:
-                tiles["codes", g] = ring.tile([P, B * F], U32, name="codes", tag="codes", bufs=3, align_bytes=64)
+                tiles["codes", g] = keep.tile([P, B * F], U32, name="codes", tag="codes%d" % (g % 2), align_bytes=64)
             src = tiles["grouped", g][:].rearrange("p b f u -> p (b f u)").bitcast(BF16)
             nc.vector.quantize_mx(
                 out=tiles["codes", g][:, m0:m1].bitcast(FP8X4), scales=out_plane[4 * g : P, m0:m1], in_=src[:, 4 * m0 : 4 * m1]
@@ -293,7 +302,7 @@ def tile_clip_class_timestep_condition_g4_kernel(
             nc.sync.dma_start(out=words_hbm[g, :, m0:m1], in_=tiles["codes", g][:, m0:m1].bitcast(I32))
 
         def store_scales(q):
-            nc.sync.dma_start(out=scales_hbm[:, 4 * q : 4 * q + 4, :], in_=out_plane[:].bitcast(I32)[32 * q : 32 * q + 16, :])
+            [nc.sync, nc.scalar][q % 2].dma_start(out=scales_hbm[:, 4 * q : 4 * q + 4, :], in_=out_plane[:].bitcast(I32)[32 * q : 32 * q + 16, :])
 
         def load_frames(f0, f1):
             nc.sync.dma_start(out=tim_sb[:, f0:f1, :], in_=time_features[:, f0:f1, :])
@@ -337,279 +346,290 @@ def tile_clip_class_timestep_condition_g4_kernel(
         def load_class():
             nc.sync.dma_start(out=cls_sb[:], in_=class_features)
 
+        def sort_frame(f, eng):
+            src = tim_sb[:, f, :].bitcast(F32).rearrange("b (s p u) -> b s u p", s=2, u=2)
+            move(eng, tim_sorted[:, SORTED.index(f), :].rearrange("b (s u p) -> b s u p", s=2, u=2), src)
+
+        def direct_cast(j, i):
+            cols = slice(ORDER[j][0] * GW, (ORDER[j][0] + 1) * GW)
+            nc.vector.tensor_tensor(
+                out=yb_tile(j)[:, :, i * P : (i + 1) * P, :],
+                in0=banks["unit", j, i][:].rearrange("b (p u e) -> b u p e", u=2, e=2),
+                in1=gain_rows[:, cols].rearrange("b (p u e) -> b u p e", u=2, e=2),
+                op=ALU.mult,
+            )
+
         fill(1)
         load_class()
         load_frames(1, 2)
-        fill(3)
-        load_frames(0, 1)
-        fill_plane(0)
-        fill(2)
         fill_plane(1)
-        load_cs(0, 2)
         load_vec(0)
+        load_frames(0, 1)
+        load_frames(2, 4)
+        fill(3)
+        load_wt(2, 3)
         build_ident()
-        load_wc(0, 2)
         narrow_ident()
         turn_class()
-        load_wt(0, 1)
-        turn_frame(1)
-        copy_class('s')
-        load_ts(0, 2)
-        quant_class(2)
-        load_vec(1)
-        turn_vec(0)
-        load_wc(2, 4)
-        turn_frame(0)
+        fill(2)
         fill(0)
-        quant_class(0)
-        copy_frame(1, 'v')
-        copy_vec(0, 's')
-        load_ts(2, 4)
+        fill_plane(0)
+        turn_vec(0)
+        load_vec(1)
+        turn_frame(1)
         warm_up()
-        spread(0, 0, 1)
-        quant_frames(1, 2)
-        copy_frame(0, 'v')
-        class_product(0)
+        copy_class('v')
+        load_cs(0, 2)
+        quant_class(3)
+        load_wc(0, 2)
+        turn_frame(0)
+        copy_frame(1, 'v')
         load_wt(1, 2)
-        load_frames(2, 4)
-        load_cs(2, 4)
-        copy_rows(0, 0, 1, 's')
-        time_product(0, 1)
-        quant_frames(0, 1)
-        add_bias(0)
+        copy_vec(0, 's')
+        turn_frame(3)
+        quant_class(0)
+        load_ts(0, 2)
+        quant_class(1)
+        copy_frame(0, 'v')
+        load_wt(0, 1)
+        load_wc(3, 4)
+        spread(0, 1, 2)
         load_frames(4, 6)
+        copy_frame(3, 'v')
         class_product(1)
+        copy_rows(0, 1, 2, 's')
+        load_cs(2, 4)
+        quant_frames(1, 2)
+        class_product(0)
+        quant_frames(0, 1)
+        spread(0, 0, 1)
+        load_wc(2, 3)
+        add_bias(1)
+        turn_frame(2)
+        load_wt(3, 4)
+        load_ts(2, 4)
+        copy_rows(0, 0, 1, 'v')
+        turn_vec(1)
+        time_product(0, 1)
+        copy_frame(2, 's')
+        add_bias(0)
+        time_product(0, 0)
+        copy_vec(1, 's')
+        quant_class(2)
+        time_product(1, 1)
         load_frames(6, 8)
         empty_unit(0, 1)
-        time_product(0, 0)
-        load_wt(2, 4)
-        turn_vec(1)
-        spread(0, 1, 2)
-        empty_unit(0, 0)
-        time_product(1, 1)
-        copy_vec(1, 's')
-        copy_rows(0, 1, 2, 's')
-        quant_class(3)
-        time_product(1, 0)
-        silu(0, 0, 2)
-        add_bias(1)
         spread(1, 0, 2)
-        empty_unit(1, 1)
-        turn_frame(2)
+        quant_frames(2, 4)
+        time_product(1, 0)
+        empty_unit(0, 0)
         copy_rows(1, 0, 2, 's')
-        turn_frame(3)
+        time_product(3, 0)
+        empty_unit(1, 1)
+        time_product(3, 1)
+        silu(0, 0, 2)
         empty_unit(1, 0)
-        copy_frame(2, 's')
         turn_frame(4)
-        apply_gain(0, 0, 2)
-        copy_frame(3, 's')
+        empty_unit(3, 0)
         turn_frame(5)
         silu(1, 0, 2)
-        quant_frames(2, 4)
-        store_y(0, 0, 2)
-        time_product(3, 1)
-        copy_frame(5, 'v')
-        copy_frame(4, 's')
-        apply_gain(1, 0, 2)
-        cast(0, 0, 2, 's')
-        time_product(3, 0)
         empty_unit(3, 1)
-        cast(1, 0, 2, 's')
-        store_y(1, 0, 2)
         turn_frame(6)
-        empty_unit(3, 0)
+        apply_gain(0, 0, 2)
+        turn_frame(7)
+        copy_frame(4, 's')
+        spread(1, 2, 4)
+        copy_frame(5, 's')
         time_product(2, 0)
-        quant_frames(4, 6)
+        apply_gain(1, 0, 2)
         silu(3, 0, 2)
         time_product(2, 1)
-        empty_unit(2, 0)
-        time_product(5, 1)
-        empty_unit(2, 1)
-        copy_frame(6, 's')
-        time_product(5, 0)
-        apply_gain(3, 0, 2)
-        time_product(4, 1)
-        silu(2, 0, 2)
-        turn_y(0, 0, 2)
-        time_product(4, 0)
-        empty_unit(5, 0)
-        cast(3, 0, 2, 's')
-        store_y(3, 0, 2)
-        empty_unit(4, 1)
-        turn_frame(7)
-        empty_unit(5, 1)
-        spread(1, 2, 4)
-        copy_y(0, 0, 128, 's')
-        empty_unit(4, 0)
-        spread(0, 2, 4)
-        copy_frame(7, 's')
-        class_product(2)
-        apply_gain(2, 0, 2)
-        silu(4, 0, 2)
-        time_product(8, 0)
-        quant_frames(6, 8)
-        copy_rows(0, 2, 4, 's')
-        store_y(2, 0, 2)
-        time_product(6, 0)
-        quant_class(1)
-        apply_gain(4, 0, 2)
+        chunk_product(3, 0, 1)
+        quant_frames(4, 6)
         copy_rows(1, 2, 4, 's')
+        store_y(1, 0, 2)
+        store_y(0, 0, 2)
+        empty_unit(2, 0)
+        cast(0, 0, 2, 'g')
+        time_product(4, 0)
+        copy_frame(6, 's')
+        empty_unit(2, 1)
+        chunk_product(3, 0, 0)
+        copy_frame(7, 's')
+        empty_unit(4, 0)
+        chunk_product(3, 0, 2)
+        chunk_silu(3, 0, 1)
+        apply_gain(3, 0, 2)
+        silu(2, 0, 2)
+        time_product(4, 1)
+        time_product(5, 1)
+        quant_frames(6, 8)
+        chunk_silu(3, 0, 0)
+        store_y(3, 0, 2)
+        chunk_product(3, 0, 3)
+        empty_unit(4, 1)
+        cast(3, 0, 2, 'g')
+        chunk_silu(3, 0, 2)
         time_product(7, 1)
-        silu(5, 0, 2)
-        add_bias(2)
-        time_product(6, 1)
-        store_y(4, 0, 2)
-        turn_y(1, 0, 2)
-        empty_unit(6, 0)
-        cast(2, 0, 2, 's')
+        empty_unit(5, 1)
+        silu(4, 0, 2)
         time_product(7, 0)
-        empty_unit(6, 1)
-        turn_y(3, 0, 2)
-        empty_unit(8, 0)
-        cast(4, 0, 2, 's')
-        chunk_product(2, 1, 1)
         empty_unit(7, 1)
+        time_product(5, 0)
+        cast(1, 1, 2, 'g')
         empty_unit(7, 0)
-        silu(6, 0, 2)
-        chunk_product(2, 1, 2)
-        apply_gain(5, 0, 2)
-        chunk_product(2, 1, 3)
-        chunk_silu(2, 1, 2)
-        copy_y(3, 0, 128, 'v')
-        chunk_product(2, 1, 0)
-        copy_y(1, 0, 128, 's')
-        store_y(5, 0, 2)
-        apply_gain(6, 0, 2)
-        silu(7, 0, 2)
-        class_product(3)
-        time_product(8, 1)
-        time_product(9, 1)
-        add_bias(3)
-        chunk_silu(2, 1, 1)
-        store_y(6, 0, 2)
-        turn_y(2, 0, 2)
-        empty_unit(8, 1)
-        chunk_silu(2, 1, 0)
-        time_product(9, 0)
-        apply_gain(7, 0, 2)
-        silu(8, 0, 2)
-        chunk_product(3, 1, 0)
-        empty_unit(9, 0)
-        chunk_silu(2, 1, 3)
-        store_y(7, 0, 2)
-        cast(5, 0, 1, 'v')
-        copy_y(2, 0, 128, 's')
-        cast(6, 0, 2, 'v')
-        turn_back(11, 0)
-        chunk_silu(3, 1, 0)
-        empty_unit(9, 1)
-        turn_y(4, 0, 2)
-        time_product(12, 1)
-        cast(7, 0, 1, 's')
-        apply_gain(8, 0, 2)
-        time_product(12, 0)
-        silu(9, 0, 2)
-        chunk_product(3, 1, 1)
-        empty_unit(11, 0)
-        store_y(8, 0, 2)
-        copy_y(4, 0, 128, 's')
-        cast(5, 1, 2, 'v')
-        turn_y(6, 0, 2)
-        cast(7, 1, 2, 'v')
-        cast(8, 0, 2, 's')
-        turn_back(10, 1)
-        empty_unit(12, 0)
-        turn_back(10, 0)
-        chunk_product(3, 1, 2)
-        empty_unit(12, 1)
-        copy_y(6, 0, 128, 's')
-        apply_gain(9, 0, 2)
-        turn_y(7, 0, 2)
-        silu(12, 0, 2)
-        turn_back(11, 1)
-        turn_y(5, 0, 2)
-        empty_unit(10, 0)
-        chunk_silu(3, 1, 1)
-        quant_y(0, 0, 512)
-        copy_y(7, 0, 128, 's')
-        empty_unit(10, 1)
-        time_product(13, 0)
-        store_codes(0, 0, 512)
-        copy_y(5, 0, 128, 's')
-        quant_y(0, 512, 1024)
-        time_product(13, 1)
-        store_y(10, 0, 2)
-        cast(10, 0, 2, 's')
-        store_y(9, 0, 2)
-        apply_gain(12, 0, 2)
         chunk_product(3, 1, 3)
-        chunk_silu(3, 1, 2)
-        empty_unit(11, 1)
-        store_y(12, 0, 2)
+        chunk_silu(3, 0, 3)
+        apply_gain(4, 0, 2)
+        cast(1, 0, 1, 's')
+        chunk_product(3, 1, 2)
+        silu(7, 0, 2)
+        time_product(9, 1)
+        apply_gain(2, 0, 2)
+        turn_back(6, 1)
         chunk_silu(3, 1, 3)
-        turn_back(14, 0)
-        empty_unit(13, 0)
-        store_y(11, 0, 2)
-        store_codes(0, 512, 1024)
-        cast(11, 0, 1, 's')
+        spread(0, 2, 3)
+        empty_unit(5, 0)
+        cast(4, 0, 2, 'g')
+        turn_back(6, 0)
+        chunk_silu(3, 1, 2)
+        chunk_product(3, 1, 0)
+        empty_unit(6, 1)
+        copy_rows(0, 2, 3, 's')
+        empty_unit(6, 0)
+        silu(5, 0, 2)
+        time_product(9, 0)
+        cast(2, 0, 2, 'g')
+        class_product(2)
+        empty_unit(9, 1)
+        time_product(11, 0)
+        store_y(6, 0, 2)
+        store_y(4, 0, 2)
+        chunk_silu(3, 1, 0)
+        empty_unit(9, 0)
+        chunk_product(2, 1, 0)
+        cast(6, 0, 2, 's')
+        add_bias(2)
+        chunk_product(2, 1, 1)
+        apply_gain(7, 0, 2)
+        silu(9, 0, 2)
+        time_product(11, 1)
+        apply_gain(5, 0, 2)
+        chunk_product(3, 1, 1)
+        store_y(7, 0, 2)
+        chunk_silu(2, 1, 1)
+        turn_back(8, 0)
+        empty_unit(11, 0)
+        cast(7, 0, 2, 'g')
+        chunk_silu(2, 1, 0)
+        turn_back(8, 1)
+        store_y(5, 0, 2)
+        store_y(2, 0, 2)
+        chunk_product(2, 1, 3)
+        empty_unit(11, 1)
+        cast(5, 0, 1, 's')
+        empty_unit(8, 1)
+        chunk_silu(3, 1, 1)
+        chunk_product(2, 1, 2)
+        cast(5, 1, 2, 'g')
+        empty_unit(8, 0)
+        silu(11, 0, 2)
+        turn_y(1, 0, 2)
+        apply_gain(9, 0, 2)
+        time_product(13, 1)
+        store_y(8, 0, 2)
+        chunk_silu(2, 1, 2)
+        turn_back(10, 0)
+        apply_gain(11, 0, 2)
+        chunk_silu(2, 1, 3)
+        turn_y(0, 0, 2)
+        store_y(9, 0, 2)
+        turn_y(4, 0, 2)
+        copy_y(1, 0, 128, 's')
+        turn_back(10, 1)
         empty_unit(13, 1)
-        turn_y(8, 0, 2)
-        cast(9, 1, 2, 's')
-        cast(9, 0, 1, 'v')
-        turn_back(15, 0)
-        empty_unit(14, 0)
+        cast(8, 0, 2, 'g')
+        turn_y(3, 0, 2)
+        copy_y(0, 0, 128, 's')
+        store_y(11, 0, 2)
+        time_product(13, 0)
+        empty_unit(10, 0)
+        cast(9, 0, 2, 's')
         turn_back(14, 1)
-        cast(12, 0, 2, 's')
-        turn_y(10, 0, 2)
-        empty_unit(15, 0)
-        empty_unit(14, 1)
+        empty_unit(10, 1)
+        turn_back(12, 1)
+        cast(11, 0, 2, 'g')
+        turn_back(12, 0)
+        empty_unit(13, 0)
+        turn_y(2, 0, 2)
+        copy_y(4, 0, 128, 's')
+        store_y(10, 0, 2)
+        empty_unit(12, 1)
+        copy_y(3, 0, 128, 's')
+        empty_unit(12, 0)
+        turn_back(14, 0)
+        cast(10, 0, 2, 'g')
         silu(13, 0, 2)
-        cast(11, 1, 2, 'v')
-        turn_y(11, 0, 2)
-        store_y(14, 0, 2)
-        cast(14, 0, 2, 'v')
-        store_y(15, 0, 1)
-        cast(15, 0, 1, 's')
+        turn_y(7, 0, 2)
+        empty_unit(14, 1)
         turn_y(9, 0, 2)
-        quant_y(1, 512, 1024)
-        copy_y(8, 0, 128, 's')
-        turn_back(15, 1)
+        store_y(12, 0, 2)
+        turn_y(5, 0, 2)
+        empty_unit(14, 0)
+        copy_y(2, 0, 128, 's')
+        turn_y(8, 0, 2)
         apply_gain(13, 0, 2)
-        store_codes(1, 512, 1024)
-        copy_y(11, 0, 128, 's')
-        turn_y(12, 0, 2)
-        copy_y(10, 0, 128, 's')
+        copy_y(7, 0, 128, 's')
+        store_y(14, 0, 2)
+        turn_y(6, 0, 2)
+        copy_y(5, 0, 128, 's')
+        turn_y(10, 0, 2)
+        quant_y(0, 0, 512)
+        copy_y(9, 0, 128, 's')
+        turn_back(15, 1)
+        quant_y(0, 512, 1024)
+        cast(13, 0, 2, 's')
+        store_codes(0, 0, 512)
+        turn_y(11, 0, 2)
         quant_y(1, 0, 512)
-        turn_y(14, 0, 2)
+        store_codes(0, 512, 1024)
+        turn_back(15, 0)
+        quant_y(1, 512, 1024)
+        cast(12, 0, 1, 's')
+        store_codes(1, 0, 512)
+        turn_y(13, 0, 2)
+        cast(12, 1, 2, 'v')
+        copy_y(6, 0, 128, 's')
+        store_codes(1, 512, 1024)
+        direct_cast(15, 1)
+        cast(14, 0, 2, 'g')
         store_y(13, 0, 2)
-        cast(13, 0, 1, 's')
+        turn_y(12, 0, 2)
+        copy_y(8, 0, 128, 's')
+        direct_cast(15, 0)
+        turn_y(15, 1, 2)
+        copy_y(10, 0, 128, 's')
         empty_unit(15, 1)
         turn_y(15, 0, 1)
-        store_codes(1, 0, 512)
-        copy_y(9, 0, 128, 's')
-        cast(13, 1, 2, 'v')
-        turn_y(13, 0, 2)
+        copy_y(12, 0, 128, 's')
+        empty_unit(15, 0)
+        turn_y(14, 0, 2)
+        copy_y(11, 0, 128, 's')
         store_y(15, 1, 2)
-        copy_y(12, 0, 128, 'v')
-        cast(15, 1, 2, 's')
-        quant_y(2, 0, 512)
-        copy_y(14, 0, 128, 's')
-        turn_y(15, 1, 2)
-        quant_y(2, 512, 1024)
-        copy_y(13, 0, 128, 's')
-        store_codes(2, 0, 512)
         copy_y(15, 0, 64, 'v')
-        store_codes(2, 512, 1024)
-        quant_y(3, 0, 256)
+        copy_y(13, 0, 128, 's')
+        quant_y(3, 0, 512)
+        store_y(15, 0, 1)
+        copy_y(14, 0, 128, 's')
+        quant_y(3, 512, 1024)
+        store_codes(3, 0, 512)
         copy_y(15, 64, 128, 's')
-        quant_y(3, 256, 512)
-        store_codes(3, 0, 256)
-        quant_y(3, 768, 1024)
-        store_codes(3, 256, 512)
-        quant_y(3, 512, 768)
-        store_codes(3, 768, 1024)
-        store_codes(3, 512, 768)
+        quant_y(2, 0, 512)
+        store_codes(3, 512, 1024)
+        quant_y(2, 512, 1024)
+        store_codes(2, 0, 512)
         store_scales(1)
-        store_scales(3)
         store_scales(0)
+        store_scales(3)
         store_scales(2)
+        store_codes(2, 512, 1024)

from contextlib import ExitStack

import concourse.mybir as mybir
from concourse.masks import make_identity

B, F, KC, KT, D = 128, 8, 512, 1024, 2048
FLOPS = 2 * B * KC * D + 2 * B * F * KT * D

F32 = mybir.dt.float32
BF16 = mybir.dt.bfloat16
U32 = mybir.dt.uint32
I32 = mybir.dt.int32
U8 = mybir.dt.uint8
FP8X4 = mybir.dt.float8_e4m3fn_x4
FP4X4 = mybir.dt.float4_e2m1fn_x4
ALU = mybir.AluOpType
ACT = mybir.ActivationFunctionType

P = 128
GW = 512
G = D // GW
PAIRS = G * F // 2
TURNED = {(3, 0): [2, 3, 4, 4], (3, 1): [6.5, 7, 8, 8.2], (2, 1): [10, 11, 12, 12]}
ORDER = [(0, 0), (1, 0), (0, 1), (1, 1), (0, 2), (1, 2), (3, 0), (0, 3), (3, 1), (1, 3), (3, 2), (2, 0), (3, 3), (2, 1), (2, 2), (2, 3)]
SORTED = []
CAST = "hhhhhhhhhhhhhhhv"


def tile_clip_class_timestep_condition_g4_kernel(
    tc, class_features, time_features, class_w_words, class_w_scales, time_w_words, time_w_scales, bias, gain, out_0, out_1, out_2
):
    nc = tc.nc
    with ExitStack() as ctx:
        keep = ctx.enter_context(tc.tile_pool(name="keep", bufs=1))
        ring = ctx.enter_context(tc.tile_pool(name="ring", bufs=3))
        psum = ctx.enter_context(tc.psum_pool(name="psum", bufs=8))
        ctx.enter_context(tc.manual_schedule())

        def bank():
            return psum.tile([P, GW], F32, name="bank", tag="bank")

        def bank_bf():
            return psum.tile([P, 2 * GW], BF16, name="bank_bf", tag="bank")

        ident = keep.tile([P, P], F32, name="ident")
        cls_sb = keep.tile([P, KC], BF16, name="cls_sb")
        tim_sb = keep.tile([P, F, KT], BF16, name="tim_sb")
        wc_words = keep.tile([P, 2 * D], U8, name="wc_words", align_bytes=64)
        wt_words = keep.tile([P, 2, 2 * D], U8, name="wt_words", align_bytes=64)
        wc_plane = keep.tile([P, D], U8, name="wc_plane", align_bytes=64)
        wt_plane = keep.tile([P, 2, D], U8, name="wt_plane", align_bytes=64)
        ident_bf = keep.tile([P, P], BF16, name="ident_bf")
        vec_squares = [keep.tile([P, P], BF16, name="bias_square"), keep.tile([P, P], BF16, name="gain_square")]
        tim_sorted = keep.tile([P, max(len(SORTED), 1), KT // 2], F32, name="tim_sorted")
        vec_cols = keep.tile([P, 2, 16], BF16, name="vec_cols")
        tim_grouped = keep.tile([P, F // 2, 2, 2, B, 2], F32, name="tim_grouped", align_bytes=64)
        warm = keep.tile([P, 8], F32, name="warm")
        bias_rows = keep.tile([P, D], BF16, name="bias_rows")
        gain_rows = keep.tile([P, D], BF16, name="gain_rows")
        vec_rows = [bias_rows, gain_rows]
        pcb = keep.tile([P, D], F32, name="pcb")
        cls_grouped = keep.tile([P, B, 2], F32, name="cls_grouped", align_bytes=64)
        reps = 4 if TURNED else 1
        cls_codes = keep.tile([P, reps * B], U32, name="cls_codes", align_bytes=64)
        cls_plane = keep.tile([P, reps * B], U8, name="cls_plane", align_bytes=64)
        tim_codes = keep.tile([P, 2, F * B], U32, name="tim_codes", align_bytes=64)
        tim_plane = keep.tile([P, 2, F * B], U8, name="tim_plane", align_bytes=64)
        out_plane = keep.tile([P, B * F], U8, name="out_plane", align_bytes=64)

        wc_hbm = class_w_words[0].bitcast(I32)
        wt_hbm = time_w_words.rearrange("s p n -> p s n").bitcast(I32)
        cs_hbm = class_w_scales[0].bitcast(I32)
        ts_hbm = time_w_scales.rearrange("s q n -> q s n").bitcast(I32)
        words_hbm = out_1.rearrange("g p m t -> g p (m t)").bitcast(I32)
        scales_hbm = out_2.bitcast(I32)

        banks = {}
        tiles = {}

        def turn_class():
            bk = bank()
            words = cls_sb[:].bitcast(F32)
            for u in range(2):
                nc.tensor.transpose(bk[:, u * B : (u + 1) * B], words[:, u : KC // 2 : 2], ident[:])
            banks["cls"] = bk

        def move(eng, dst, src):
            if eng == "s":
                nc.scalar.copy(out=dst, in_=src)
            else:
                nc.vector.tensor_copy(out=dst, in_=src)

        def copy_class(eng):
            move(eng, cls_grouped[:], banks["cls"][:, 0 : 2 * B].rearrange("p (u b) -> p b u", u=2))

        def quant_class(r):
            cols = slice(r * B, (r + 1) * B)
            nc.vector.quantize_mx(
                out=cls_codes[:, cols].bitcast(FP8X4),
                scales=cls_plane[:, cols],
                in_=cls_grouped[:].rearrange("p b u -> p (b u)").bitcast(BF16),
            )

        def turn_frame(f):
            bk = bank()
            words = tim_sb[:, f, :].bitcast(F32)
            for s in range(2):
                for u in range(2):
                    k = 2 * s + u
                    if f in SORTED:
                        src = tim_sorted[:, SORTED.index(f), k * P : (k + 1) * P]
                    else:
                        src = words[:, 256 * s + u : 256 * (s + 1) : 2]
                    nc.tensor.transpose(bk[:, k * B : (k + 1) * B], src, ident[:])
            banks["frame", f] = bk

        def copy_frame(f, eng):
            dst = tim_grouped[:, f // 2, :, f % 2, :, :]
            src = banks["frame", f][:].rearrange("p (s u b) -> p s b u", s=2, u=2)
            if eng == "s":
                nc.scalar.copy(out=dst, in_=src)
            else:
                nc.vector.tensor_copy(out=dst, in_=src)

        def quant_frames(f0, f1):
            cols = slice(f0 * B, f1 * B)
            for s in range(2):
                src = tim_grouped[:, f0 // 2, s, f0 % 2 : f0 % 2 + f1 - f0, :, :]
                nc.vector.quantize_mx(
                    out=tim_codes[:, s, cols].bitcast(FP8X4),
                    scales=tim_plane[:, s, cols],
                    in_=src.rearrange("p i b u -> p (i b u)").bitcast(BF16),
                )

        def turn_vec(which):
            bk = bank_bf()
            nc.tensor.transpose(bk[:, 0:P], vec_squares[which][:], ident_bf[:])
            banks["vec", which] = bk

        def copy_vec(which, eng):
            move(eng, vec_cols[:, which, :], banks["vec", which][:, 0:16])

        def spread(which, g0, g1):
            bk = bank_bf()
            for c in range(4 * (g1 - g0)):
                k = 4 * g0 + c
                nc.tensor.transpose(bk[:, c * P : (c + 1) * P], vec_cols[:, which, k : k + 1].to_broadcast([P, P]), ident_bf[:])
            banks["spread", which, g0] = bk

        def copy_rows(which, g0, g1, eng):
            move(eng, vec_rows[which][:, g0 * GW : g1 * GW], banks["spread", which, g0][:, 0 : (g1 - g0) * GW])

        def class_product(g):
            bk = bank()
            nc.tensor.matmul_mx(
                out=bk[:],
                lhsT=cls_codes[:, 0:B].bitcast(FP8X4),
                lhsT_scale=cls_plane[:, 0:B],
                rhs=wc_words[:, 2 * GW * g : 2 * GW * (g + 1)].bitcast(FP4X4),
                rhs_scale=wc_plane[:, GW * g : GW * (g + 1)],
                start=True,
                stop=True,
            )
            banks["pc", g] = bk

        def add_bias(g):
            nc.vector.tensor_tensor(out=pcb[:, g * GW : (g + 1) * GW], in0=banks["pc", g][:], in1=bias_rows[:, g * GW : (g + 1) * GW], op=ALU.add)

        def is_turned(j):
            return (ORDER[j][0], ORDER[j][1] // 2) in TURNED

        def time_product(j, i):
            g = ORDER[j][0]
            f = 2 * ORDER[j][1] + i
            bk = bank()
            for s in range(2):
                nc.tensor.matmul_mx(
                    out=bk[:],
                    lhsT=tim_codes[:, s, f * B : (f + 1) * B].bitcast(FP8X4),
                    lhsT_scale=tim_plane[:, s, f * B : (f + 1) * B],
                    rhs=wt_words[:, s, 2 * GW * g : 2 * GW * (g + 1)].bitcast(FP4X4),
                    rhs_scale=wt_plane[:, s, GW * g : GW * (g + 1)],
                    start=(s == 0),
                    stop=(s == 1),
                )
            banks["unit", j, i] = bk

        def chunk_product(g, h, c):
            bk = bank()
            d0 = GW * g + P * c
            toks = slice(4 * B * h, 4 * B * (h + 1))
            nc.tensor.matmul_mx(
                out=bk[:],
                lhsT=wc_words[:, 2 * d0 : 2 * (d0 + P)].bitcast(FP4X4),
                lhsT_scale=wc_plane[:, d0 : d0 + P],
                rhs=cls_codes[:].bitcast(FP8X4),
                rhs_scale=cls_plane[:],
                start=True,
                stop=False,
            )
            for s in range(2):
                nc.tensor.matmul_mx(
                    out=bk[:],
                    lhsT=wt_words[:, s, 2 * d0 : 2 * (d0 + P)].bitcast(FP4X4),
                    lhsT_scale=wt_plane[:, s, d0 : d0 + P],
                    rhs=tim_codes[:, s, toks].bitcast(FP8X4),
                    rhs_scale=tim_plane[:, s, toks],
                    start=False,
                    stop=(s == 1),
                )
            banks["chunk", g, h, c] = bk

        def chunk_silu(g, h, c):
            if ("turned", g, h) not in tiles:
                tiles["turned", g, h] = ring.tile([P, 4, GW], F32, name="turned", tag="turned", bufs=3)
            k = 4 * g + c
            nc.scalar.activation(
                out=tiles["turned", g, h][:, c, :], in_=banks["chunk", g, h, c][:], func=ACT.Silu, bias=vec_cols[:, 0, k : k + 1]
            )

        def turn_back(j, i):
            g, h = ORDER[j][0], ORDER[j][1] // 2
            fl = 2 * (ORDER[j][1] % 2) + i
            bk = bank()
            for c in range(4):
                nc.tensor.transpose(bk[:, c * P : (c + 1) * P], tiles["turned", g, h][:, c, fl * B : (fl + 1) * B], ident[:])
            banks["unit", j, i] = bk

        def y_tile(j):
            if ("y", j) not in tiles:
                tiles["y", j] = keep.tile([P, 2, GW], F32, name="y%d" % j)
            return tiles["y", j]

        def yb_tile(j):
            if ("yb", j) not in tiles:
                tiles["yb", j] = keep.tile([P, 2, 2 * P, 2], BF16, name="yb", tag="yb%d" % (j % 8))
            return tiles["yb", j]

        def empty_unit(j, i):
            cols = slice(ORDER[j][0] * GW, (ORDER[j][0] + 1) * GW)
            if is_turned(j):
                nc.vector.tensor_tensor(out=y_tile(j)[:, i, :], in0=banks["unit", j, i][:], in1=gain_rows[:, cols], op=ALU.mult)
            else:
                nc.vector.tensor_tensor(out=y_tile(j)[:, i, :], in0=banks["unit", j, i][:], in1=pcb[:, cols], op=ALU.add)

        def silu(j, i0, i1):
            z = tiles["y", j][:, i0:i1, :].rearrange("p i d -> p (i d)")
            nc.scalar.activation(out=z, in_=z, func=ACT.Silu)

        def apply_gain(j, i0, i1):
            cols = slice(ORDER[j][0] * GW, (ORDER[j][0] + 1) * GW)
            nc.vector.tensor_tensor(
                out=y_tile(j)[:, i0:i1, :],
                in0=tiles["y", j][:, i0:i1, :],
                in1=gain_rows[:, cols].unsqueeze(1).to_broadcast([P, i1 - i0, GW]),
                op=ALU.mult,
            )

        def store_y(j, i0, i1):
            g, f0 = ORDER[j][0], 2 * ORDER[j][1]
            nc.sync.dma_start(out=out_0[:, f0 + i0 : f0 + i1, g * GW : (g + 1) * GW], in_=tiles["y", j][:, i0:i1, :])

        def cast(j, i0, i1, eng):
            dst = yb_tile(j)[:, :, i0 * P : i1 * P, :]
            src = tiles["y", j][:, i0:i1, :].rearrange("b i (p u e) -> b u (i p) e", u=2, e=2)
            if eng == "g":
                nc.gpsimd.tensor_scalar(out=dst, in0=src, scalar1=1.0, scalar2=1.0, op0=ALU.mult, op1=ALU.mult)
            elif eng == "s":
                nc.scalar.copy(out=dst, in_=src)
            else:
                nc.vector.tensor_copy(out=dst, in_=src)

        def turn_y(j, i0, i1):
            if ("yt", j) not in banks:
                banks["yt", j] = bank()
            words = tiles["yb", j][:].rearrange("b u c e -> b (u c e)").bitcast(F32)
            for i in range(i0, i1):
                for u in range(2):
                    k = 2 * u + i
                    nc.tensor.transpose(banks["yt", j][:, k * P : (k + 1) * P], words[:, k * P : (k + 1) * P], ident[:])

        def copy_y(j, b0, b1, eng):
            g, f0 = ORDER[j][0], 2 * ORDER[j][1]
            if ("grouped", g) not in tiles:
                tiles["grouped", g] = ring.tile([P, B, F, 2], F32, name="grouped", tag="grouped", bufs=4, align_bytes=64)
            dst = tiles["grouped", g][:, b0:b1, f0 : f0 + 2, :]
            src = banks["yt", j][:].rearrange("p (u i b) -> p b i u", u=2, i=2)[:, b0:b1, :, :]
            if eng == "s":
                nc.scalar.copy(out=dst, in_=src)
            else:
                nc.vector.tensor_copy(out=dst, in_=src)

        def quant_y(g, m0, m1):
            if ("codes", g) not in tiles:
                tiles["codes", g] = keep.tile([P, B * F], U32, name="codes", tag="codes%d" % (g % 2), align_bytes=64)
            src = tiles["grouped", g][:].rearrange("p b f u -> p (b f u)").bitcast(BF16)
            nc.vector.quantize_mx(
                out=tiles["codes", g][:, m0:m1].bitcast(FP8X4), scales=out_plane[4 * g : P, m0:m1], in_=src[:, 4 * m0 : 4 * m1]
            )

        def store_codes(g, m0, m1):
            nc.sync.dma_start(out=words_hbm[g, :, m0:m1], in_=tiles["codes", g][:, m0:m1].bitcast(I32))

        def store_scales(q):
            [nc.sync, nc.scalar][q % 2].dma_start(out=scales_hbm[:, 4 * q : 4 * q + 4, :], in_=out_plane[:].bitcast(I32)[32 * q : 32 * q + 16, :])

        def load_frames(f0, f1):
            nc.sync.dma_start(out=tim_sb[:, f0:f1, :], in_=time_features[:, f0:f1, :])

        def load_wc(g0, g1):
            cols = slice(256 * g0, 256 * g1)
            nc.sync.dma_start(out=wc_words[:].bitcast(I32)[:, cols], in_=wc_hbm[:, cols])

        def load_wt(g0, g1):
            cols = slice(256 * g0, 256 * g1)
            nc.sync.dma_start(out=wt_words[:].bitcast(I32)[:, :, cols], in_=wt_hbm[:, :, cols])

        def load_cs(g0, g1):
            cols = slice(128 * g0, 128 * g1)
            for q in range(4):
                nc.sync.dma_start(out=wc_plane[:].bitcast(I32)[32 * q : 32 * q + 4, cols], in_=cs_hbm[4 * q : 4 * q + 4, cols])

        def load_ts(g0, g1):
            cols = slice(128 * g0, 128 * g1)
            for q in range(4):
                nc.sync.dma_start(out=wt_plane[:].bitcast(I32)[32 * q : 32 * q + 4, :, cols], in_=ts_hbm[4 * q : 4 * q + 4, :, cols])

        def load_vec(which):
            nc.sync.dma_start(out=vec_squares[which][0:16, :], in_=[bias, gain][which].rearrange("(c p) -> c p", p=P))

        def fill(k):
            nc.vector.memset([warm[:], vec_squares[0][:], vec_squares[1][:], ident[:]][k], 0.0)

        def fill_plane(k):
            nc.vector.memset([wc_plane[:], wt_plane[:].rearrange("p s n -> p (s n)")][k].bitcast(I32), 0)

        def build_ident():
            make_identity(nc, ident[:], True)

        def narrow_ident():
            nc.vector.tensor_copy(out=ident_bf[:], in_=ident[:])

        def warm_up():
            nc.scalar.activation(out=warm[:], in_=warm[:], func=ACT.Silu)

        def load_class():
            nc.sync.dma_start(out=cls_sb[:], in_=class_features)

        def sort_frame(f, eng):
            src = tim_sb[:, f, :].bitcast(F32).rearrange("b (s p u) -> b s u p", s=2, u=2)
            move(eng, tim_sorted[:, SORTED.index(f), :].rearrange("b (s u p) -> b s u p", s=2, u=2), src)

        def direct_cast(j, i):
            cols = slice(ORDER[j][0] * GW, (ORDER[j][0] + 1) * GW)
            nc.vector.tensor_tensor(
                out=yb_tile(j)[:, :, i * P : (i + 1) * P, :],
                in0=banks["unit", j, i][:].rearrange("b (p u e) -> b u p e", u=2, e=2),
                in1=gain_rows[:, cols].rearrange("b (p u e) -> b u p e", u=2, e=2),
                op=ALU.mult,
            )

        fill(1)
        load_class()
        load_frames(1, 2)
        fill_plane(1)
        load_vec(0)
        load_frames(0, 1)
        load_frames(2, 4)
        fill(3)
        load_wt(2, 3)
        build_ident()
        narrow_ident()
        turn_class()
        fill(2)
        fill(0)
        fill_plane(0)
        turn_vec(0)
        load_vec(1)
        turn_frame(1)
        warm_up()
        copy_class('v')
        load_cs(0, 2)
        quant_class(3)
        load_wc(0, 2)
        turn_frame(0)
        copy_frame(1, 'v')
        load_wt(1, 2)
        copy_vec(0, 's')
        turn_frame(3)
        quant_class(0)
        load_ts(0, 2)
        quant_class(1)
        copy_frame(0, 'v')
        load_wt(0, 1)
        load_wc(3, 4)
        spread(0, 1, 2)
        load_frames(4, 6)
        copy_frame(3, 'v')
        class_product(1)
        copy_rows(0, 1, 2, 's')
        load_cs(2, 4)
        quant_frames(1, 2)
        class_product(0)
        quant_frames(0, 1)
        spread(0, 0, 1)
        load_wc(2, 3)
        add_bias(1)
        turn_frame(2)
        load_wt(3, 4)
        load_ts(2, 4)
        copy_rows(0, 0, 1, 'v')
        turn_vec(1)
        time_product(0, 1)
        copy_frame(2, 's')
        add_bias(0)
        time_product(0, 0)
        copy_vec(1, 's')
        quant_class(2)
        time_product(1, 1)
        load_frames(6, 8)
        empty_unit(0, 1)
        spread(1, 0, 2)
        quant_frames(2, 4)
        time_product(1, 0)
        empty_unit(0, 0)
        copy_rows(1, 0, 2, 's')
        time_product(3, 0)
        empty_unit(1, 1)
        time_product(3, 1)
        silu(0, 0, 2)
        empty_unit(1, 0)
        turn_frame(4)
        empty_unit(3, 0)
        turn_frame(5)
        silu(1, 0, 2)
        empty_unit(3, 1)
        turn_frame(6)
        apply_gain(0, 0, 2)
        turn_frame(7)
        copy_frame(4, 's')
        spread(1, 2, 4)
        copy_frame(5, 's')
        time_product(2, 0)
        apply_gain(1, 0, 2)
        silu(3, 0, 2)
        time_product(2, 1)
        chunk_product(3, 0, 1)
        quant_frames(4, 6)
        copy_rows(1, 2, 4, 's')
        store_y(1, 0, 2)
        store_y(0, 0, 2)
        empty_unit(2, 0)
        cast(0, 0, 2, 'g')
        time_product(4, 0)
        copy_frame(6, 's')
        empty_unit(2, 1)
        chunk_product(3, 0, 0)
        copy_frame(7, 's')
        empty_unit(4, 0)
        chunk_product(3, 0, 2)
        chunk_silu(3, 0, 1)
        apply_gain(3, 0, 2)
        silu(2, 0, 2)
        time_product(4, 1)
        time_product(5, 1)
        quant_frames(6, 8)
        chunk_silu(3, 0, 0)
        store_y(3, 0, 2)
        chunk_product(3, 0, 3)
        empty_unit(4, 1)
        cast(3, 0, 2, 'g')
        chunk_silu(3, 0, 2)
        time_product(7, 1)
        empty_unit(5, 1)
        silu(4, 0, 2)
        time_product(7, 0)
        empty_unit(7, 1)
        time_product(5, 0)
        cast(1, 1, 2, 'g')
        empty_unit(7, 0)
        chunk_product(3, 1, 3)
        chunk_silu(3, 0, 3)
        apply_gain(4, 0, 2)
        cast(1, 0, 1, 's')
        chunk_product(3, 1, 2)
        silu(7, 0, 2)
        time_product(9, 1)
        apply_gain(2, 0, 2)
        turn_back(6, 1)
        chunk_silu(3, 1, 3)
        spread(0, 2, 3)
        empty_unit(5, 0)
        cast(4, 0, 2, 'g')
        turn_back(6, 0)
        chunk_silu(3, 1, 2)
        chunk_product(3, 1, 0)
        empty_unit(6, 1)
        copy_rows(0, 2, 3, 's')
        empty_unit(6, 0)
        silu(5, 0, 2)
        time_product(9, 0)
        cast(2, 0, 2, 'g')
        class_product(2)
        empty_unit(9, 1)
        time_product(11, 0)
        store_y(6, 0, 2)
        store_y(4, 0, 2)
        chunk_silu(3, 1, 0)
        empty_unit(9, 0)
        chunk_product(2, 1, 0)
        cast(6, 0, 2, 's')
        add_bias(2)
        chunk_product(2, 1, 1)
        apply_gain(7, 0, 2)
        silu(9, 0, 2)
        time_product(11, 1)
        apply_gain(5, 0, 2)
        chunk_product(3, 1, 1)
        store_y(7, 0, 2)
        chunk_silu(2, 1, 1)
        turn_back(8, 0)
        empty_unit(11, 0)
        cast(7, 0, 2, 'g')
        chunk_silu(2, 1, 0)
        turn_back(8, 1)
        store_y(5, 0, 2)
        store_y(2, 0, 2)
        chunk_product(2, 1, 3)
        empty_unit(11, 1)
        cast(5, 0, 1, 's')
        empty_unit(8, 1)
        chunk_silu(3, 1, 1)
        chunk_product(2, 1, 2)
        cast(5, 1, 2, 'g')
        empty_unit(8, 0)
        silu(11, 0, 2)
        turn_y(1, 0, 2)
        apply_gain(9, 0, 2)
        time_product(13, 1)
        store_y(8, 0, 2)
        chunk_silu(2, 1, 2)
        turn_back(10, 0)
        apply_gain(11, 0, 2)
        chunk_silu(2, 1, 3)
        turn_y(0, 0, 2)
        store_y(9, 0, 2)
        turn_y(4, 0, 2)
        copy_y(1, 0, 128, 's')
        turn_back(10, 1)
        empty_unit(13, 1)
        cast(8, 0, 2, 'g')
        turn_y(3, 0, 2)
        copy_y(0, 0, 128, 's')
        store_y(11, 0, 2)
        time_product(13, 0)
        empty_unit(10, 0)
        cast(9, 0, 2, 's')
        turn_back(14, 1)
        empty_unit(10, 1)
        turn_back(12, 1)
        cast(11, 0, 2, 'g')
        turn_back(12, 0)
        empty_unit(13, 0)
        turn_y(2, 0, 2)
        copy_y(4, 0, 128, 's')
        store_y(10, 0, 2)
        empty_unit(12, 1)
        copy_y(3, 0, 128, 's')
        empty_unit(12, 0)
        turn_back(14, 0)
        cast(10, 0, 2, 'g')
        silu(13, 0, 2)
        turn_y(7, 0, 2)
        empty_unit(14, 1)
        turn_y(9, 0, 2)
        store_y(12, 0, 2)
        turn_y(5, 0, 2)
        empty_unit(14, 0)
        copy_y(2, 0, 128, 's')
        turn_y(8, 0, 2)
        apply_gain(13, 0, 2)
        copy_y(7, 0, 128, 's')
        store_y(14, 0, 2)
        turn_y(6, 0, 2)
        copy_y(5, 0, 128, 's')
        turn_y(10, 0, 2)
        quant_y(0, 0, 512)
        copy_y(9, 0, 128, 's')
        turn_back(15, 1)
        quant_y(0, 512, 1024)
        cast(13, 0, 2, 's')
        store_codes(0, 0, 512)
        turn_y(11, 0, 2)
        quant_y(1, 0, 512)
        store_codes(0, 512, 1024)
        turn_back(15, 0)
        quant_y(1, 512, 1024)
        cast(12, 0, 1, 's')
        store_codes(1, 0, 512)
        turn_y(13, 0, 2)
        cast(12, 1, 2, 'v')
        copy_y(6, 0, 128, 's')
        store_codes(1, 512, 1024)
        direct_cast(15, 1)
        cast(14, 0, 2, 'g')
        store_y(13, 0, 2)
        turn_y(12, 0, 2)
        copy_y(8, 0, 128, 's')
        direct_cast(15, 0)
        turn_y(15, 1, 2)
        copy_y(10, 0, 128, 's')
        empty_unit(15, 1)
        turn_y(15, 0, 1)
        copy_y(12, 0, 128, 's')
        empty_unit(15, 0)
        turn_y(14, 0, 2)
        copy_y(11, 0, 128, 's')
        store_y(15, 1, 2)
        copy_y(15, 0, 64, 'v')
        copy_y(13, 0, 128, 's')
        quant_y(3, 0, 512)
        store_y(15, 0, 1)
        copy_y(14, 0, 128, 's')
        quant_y(3, 512, 1024)
        store_codes(3, 0, 512)
        copy_y(15, 64, 128, 's')
        quant_y(2, 0, 512)
        store_codes(3, 512, 1024)
        quant_y(2, 512, 1024)
        store_codes(2, 0, 512)
        store_scales(1)
        store_scales(0)
        store_scales(3)
        store_scales(2)
        store_codes(2, 512, 1024)
